import numpy as np, ml_dtypes
CORES = [40,64,80,88,96,104,120,144]
N = 8
import mx_ref
BF = ml_dtypes.bfloat16
def gentries(a):
    return np.ascontiguousarray(a.reshape(8, 16, -1).transpose(0, 2, 1)).reshape(8, -1)
def gtable(e):
    e = np.asarray(e); return np.ascontiguousarray(e.reshape(8, -1, 16).transpose(0, 2, 1)).reshape(128, -1).astype(np.int32)
def gcols(t, e):
    v = np.concatenate([t.reshape(8, 16, -1, 4), np.zeros((8, 16, 1, 4), BF)], axis=2)
    return np.ascontiguousarray(np.stack([v[g][:, e[g]] for g in range(8)])).reshape(128, -1)
def gpick(z, e):
    return np.concatenate([z[16 * g:16 * g + 16][:, e[g]] for g in range(8)])
def tile(rs):
    return np.stack(rs, axis=2).reshape(128, -1).astype(BF)
def pick(q, e):
    c = np.concatenate([q[0].reshape(128, -1, 4), np.zeros((128, 1, 4), np.uint8)], axis=1); s = np.concatenate([q[1], np.ones((16, 1), np.uint8)], axis=1)
    return (np.ascontiguousarray(c[:, e].reshape(128, -1)), np.ascontiguousarray(s[:, e]))
def join(*qs):
    return (np.concatenate([q[0] for q in qs], axis=1), np.concatenate([q[1] for q in qs], axis=1))
def put(q, e, v):
    c, s = q[0].reshape(128, -1, 4).copy(), q[1].copy(); c[:, e] = v[0].reshape(128, -1, 4); s[:, e] = v[1]
    return (c.reshape(128, -1), s)
def pk(c, s):
    return (np.ascontiguousarray(c), mx_ref.live(s))
def emit(q):
    return q[0], q[1]
def packed(v, rng):
    q = [mx_ref.quantize(np.ascontiguousarray(v[r])) for r in range(N)]
    return np.stack([a for a, b in q]), np.stack([mx_ref.plane(b, rng) for a, b in q])
def values_of_codes():
    e, c = np.zeros((128, 128, 4), np.float32), np.zeros((128, 2, 4), np.uint8)
    e[np.arange(128), np.arange(128), 0] = 1
    c[:127, :, 0] = np.arange(256).reshape(2, 128).T[:127]
    return mx_ref.matmul(mx_ref.quantize(e.reshape(128, 512).astype(BF)), (c.reshape(128, 8), np.full((16, 2), 127, np.uint8))).T.reshape(-1).astype(np.float64)
CODE_VALUE, SCALE_VALUE = values_of_codes(), 2.0 ** (np.arange(256) - 127.0)
def decode(q):
    return (CODE_VALUE[q[0]].reshape(16, 8, -1, 4) * SCALE_VALUE[q[1]][:, None, :, None] + 0.0).reshape(128, -1).astype(np.float32)
def f(rng, *shape):
    return mx_ref.flush((rng.standard_normal(shape, dtype=np.float32) * np.exp2(rng.integers(-2, 3, shape[:-1] + (1,)))).astype(BF))
def wide(rng, *shape, cols=0):
    v = rng.standard_normal(shape, dtype=np.float32) * np.exp2(rng.integers(-12, 13, shape)).astype(np.float32)
    if cols: v *= np.repeat(np.exp2(rng.integers(-cols, cols + 1, shape[:-2] + (1, shape[-1] // 4))) * (rng.random(shape[:-2] + (1, shape[-1] // 4)) > 0.0625), 4, axis=-1).astype(np.float32)
    return mx_ref.flush(v.astype(BF))
C = 288
STEP = [4, 1, 2]
def numbers_of(rng):
    return {"x": np.array(f(rng, N, 128, 4 * C)), "u": np.array(f(rng, N, 128, 512)), "v": np.array(f(rng, N, 128, 512))}
def drawn(rng):
    e = np.tile(np.arange(C), (N, 8, 1))
    p, k, s, m = rng.permuted(e, axis=2), rng.permuted(e, axis=2), rng.permuted(e, axis=2), np.zeros_like(e)
    np.put_along_axis(m, s[:, :, ::2], s[:, :, 1::2], 2)
    np.put_along_axis(m, s[:, :, 1::2], s[:, :, ::2], 2)
    return p, k, m
def stored(p, k, m):
    return {"pg": np.stack([gtable(p[r]) for r in range(N)]), "kg": np.stack([gtable(k[r]) for r in range(N)]), "mg": np.stack([gtable(m[r]) for r in range(N)])}
def layers(rng):
    return np.array(f(rng, N, 128, 2048)).reshape(N, 8, 16, 4, 8, 16, 4)
def weights(rng, w):
    c, s = packed(np.ascontiguousarray(w).reshape(N, 128, 2048), rng)
    return {"wc": c, "ws": s}
def setup_inputs(rng):
    return {**numbers_of(rng), **stored(*drawn(rng)), **weights(rng, layers(rng))}
def setup_inputs_ties(rng):
    d = numbers_of(rng)
    o = rng.permutation(N)
    s = rng.integers(-1, 2, (N, 2, 8, C))
    s[o[0]] = 0
    s[o[1]] = 1
    s[o[2], 0] = np.where(np.arange(C) % 2 == 1, 1, rng.integers(-1, 1, (8, C)))
    x = d["x"].astype(np.float32).reshape(N, 8, 16, C, 4)
    u = d["u"].astype(np.float32).reshape(N, 128, 128, 4)
    for i in range(2):
        x[:, :, i] = 0
        x[:, :, i, :, 0] = s[:, i]
        u[:, :, i::16] = 0
        for h in range(0, 128, 16): u[:, h + i, h + i, 0] = 1
    p, k, m = drawn(rng)
    p[o[2]] = k[o[2]] = np.arange(C)
    m[o[2]] = np.arange(C) ^ 1
    w = layers(rng)
    w[:, :, :, :, :, :8] = 0
    return {"x": x.reshape(N, 128, 4 * C).astype(BF), "u": u.reshape(N, 128, 512).astype(BF), "v": d["v"], **stored(p, k, m), **weights(rng, w)}
def setup_inputs_near(rng):
    d = numbers_of(rng)
    o = rng.permutation(N)
    k = np.where(o % 2 == 0, 2.0 ** -30, 1.0)
    x = np.zeros((N, 8, 16, C, 4))
    s = rng.integers(-1, 2, (N, 2, 8, C)) * k[:, None, None, None]
    for i in range(2):
        x[:, :, 2 * i, :, 0] = 1.125 * s[:, i]
        x[:, :, 2 * i + 1, :, 0] = -1.25 * s[:, i]
    x[:, :, 9, :, 0] = rng.choice([-1.0, 1.0], (N, 8, C)) * 2.0 ** -17
    x[:, :, 10:] = rng.choice([-1.0, 1.0], (N, 8, 6, C, 4)) * (1 + 0.125 * rng.integers(0, 8, (N, 8, 6, C, 4))) * np.exp2(-12.0 - rng.integers(0, 4, (N, 8, 6, C, 4)))
    u = d["u"].astype(np.float32).reshape(N, 128, 128, 4)
    u[:, :, ::16] = 0
    u[:, :, 1::16] = 0
    w = layers(rng)
    w[:, :, :8] = 0
    w[:, :, :, :, :, :10] = 0
    for r in range(N):
        for g in rng.permutation(8)[:4]: x[r, g, 0, rng.integers(C), 0] = 2.0 ** 30 * rng.choice([-1.0, 1.0])
        if o[r] == 0:
            x[r, :, :8] = 0
            x[r, :, 0, :, 0] = 2.0 ** -30
        for g in range(8):
            h = 16 * g
            if o[r] == 0:
                u[r, h + 4, h, 0] = 2.0 ** -30
                u[r, h + 4, h + 1, 0] = -2.0 ** -30
                w[r, g, 8, 0, g, 4, 0] = 2.0 ** -8
                w[r, g, 9, 0, g, 4, 0] = 2.0 ** -22
            else:
                for i in range(2):
                    u[r, h + 2 * i, h + i, 0] = 1.125 * k[r]
                    u[r, h + 2 * i + 1, h + i, 0] = k[r]
    return {"x": x.astype(np.float32).reshape(N, 128, 4 * C).astype(BF), "u": u.reshape(N, 128, 512).astype(BF), "v": d["v"], **stored(*drawn(rng)), **weights(rng, w)}
def setup_inputs_odd(rng):
    d = numbers_of(rng)
    x = (1.0 + (2 * rng.integers(0, 64, (N, 16, 8, C, 4)) + 1) * 2.0 ** -7) * np.exp2(-rng.integers(0, 7, (N, 16, 8, C, 4)).astype(np.float64)) * rng.choice([-1.0, 1.0], (N, 16, 8, C, 4))
    x[:, ::2, 0, :, 0] = 1.96875 * 2.0 ** 8 * rng.choice([-1.0, 1.0], (8, 1))
    x[:, 1::2, 0, :, 0] = 1.96875 * 2.0 ** 8 * rng.choice([-1.0, 1.0], (N, 8, C))
    u = d["u"].astype(np.float32).reshape(N, 16, 8, 128, 4)
    u[:, :, 0, ::16] = 0
    u[:, :, :, 1::16] = 0
    h = rng.permutation(8) % 4
    for g in range(8):
        x[:, 2 * g, 1, :, 0] = (8 + rng.integers(0, 2, (N, C))) * 2.0 ** (int(h[g]) - 9)
        x[:, 2 * g, 2, :, 0] = -2.0 ** (int(h[g]) - 6)
        u[:, 2 * g, 1:3, 16 * g + 1, 0] = 1
    w = layers(rng)
    for i in (0, 8):
        w[:, :, i] = 0
        w[:, :, :, :, :, i] = 0
    w[:, :, :, 0, :, 1:3] = 0
    for g in range(8): w[:, g, 0, 0, g, 0, 0] = -0.5
    p, k, m = drawn(rng)
    t = int(rng.integers(N))
    p[t] = m[t] = np.arange(C)
    k[t] = rng.permutation(C)
    return {"x": x.astype(np.float32).reshape(N, 128, 4 * C).astype(BF), "u": u.reshape(N, 128, 512).astype(BF), "v": d["v"], **stored(p, k, m), **weights(rng, w)}
def setup_inputs_ends(rng):
    d = numbers_of(rng)
    o, ep, ek, em = [rng.permutation(N) % 4 for i in range(4)]
    s = rng.choice([-1.0, 1.0], (N, 128, C, 4))
    s[o == 0] = -1
    s[o == 1] = rng.choice([-1.0, 1.0], (N, 1, C, 1))[o == 1]
    x = s * (0.90 + 0.02 * rng.random((N, 128, C, 4))) * 2.0 ** 30
    tiny = (1 + 0.125 * rng.integers(0, 8, (N, 128, C, 4))) * 2.0 ** -30
    x[o == 3] = (s * tiny)[o == 3]
    x[:, 8:16] = tiny[:, 8:16]
    u = d["u"].astype(np.float32).reshape(N, 128, 128, 4)
    for r in range(N):
        h = rng.permutation(8)
        size = 2.0 ** -30 if o[r] == 3 else 2.0 ** 30
        u[r, :, ::16] = ((h % 2 * 2 - 1) * size)[None, :, None]
        u[r, :, 1::16] = ((h // 2 % 2 * 2 - 1) * size)[None, :, None]
    v = rng.choice([-1.0, 1.0], (N, 128, 512)) * np.where(o % 2 == 0, 2.0 ** 30, 2.0 ** -30)[:, None, None]
    p, k, m = drawn(rng)
    line = np.arange(C)
    p[ep == 0] = line
    p[ep == 1] = (line + 1) % C
    p[ep == 2] = C - 1 - line
    k[ek == 0] = line
    k[ek == 1] = C - 1 - line
    k[ek == 2] = (line + C - 1) % C
    m[em == 0] = line
    m[em == 1] = C - 1 - line
    m[em == 2] = line ^ 1
    w = np.zeros((N, 128, 4, 128, 4), np.float32)
    i = np.arange(128)
    for b in range(4): w[:, i, b, i, b] = np.where((i >= 8) & (i < 16), np.where(o == 3, 2.0 ** 8, 2.0 ** -8)[:, None], -0.25)
    return {"x": x.astype(np.float32).reshape(N, 128, 4 * C).astype(BF), "u": u.reshape(N, 128, 512).astype(BF), "v": v.astype(np.float32).astype(BF), **stored(p, k, m), **weights(rng, w.astype(BF))}
def setup_inputs_spread(rng):
    d = setup_inputs(rng)
    d["x"] = wide(rng, N, 128, 4 * C, cols=6)
    return d
def check_inputs(d):
    b = []
    for k in ("x", "u", "v"):
        a = np.abs(d[k].astype(np.float32))
        if not (np.isfinite(a).all() and ((a == 0) | (a >= 2.0 ** -30) & (a <= 2.0 ** 30)).all()): b.append("a value of " + k)
    none, least, most = [emit(mx_ref.quantize(np.full((128, 16), k, np.float32).astype(BF)))[1][0, 0] for k in (0.0, 2.0 ** -8, 2.0 ** 8)]
    top = emit(mx_ref.quantize(np.full((128, 16), 1.9921875, np.float32).astype(BF)))[0][0, 0] & 0x7F
    line = np.arange(C)
    for r in range(N):
        for k in ("pg", "kg"):
            if not (np.sort(gentries(d[k][r]), axis=1) == line).all(): b.append(k + ": no permutation")
        m = gentries(d["mg"][r])
        if not ((m >= 0) & (m < C)).all(): b.append("an entry of mg")
        elif not (np.take_along_axis(m, m, 1) == line).all(): b.append("mg: a mate's mate")
        if ((d["wc"][r] == 0x7F) | (d["wc"][r] == 0xFF)).any(): b.append("wc: a code that is no number")
        if ((d["wc"][r] & 0x7F) > top).any(): b.append("wc: a code that quantize_mx does not give")
        s = mx_ref.live(d["ws"][r])
        if ((s != none) & ((s < least) | (s > most))).any(): b.append("ws: a scale out of range")
    return b
def reference(x, u, v, pg, kg, mg, wc, ws):
    qu = [mx_ref.quantize(u[r]) for r in range(N)]
    lay = [pk(wc[r], ws[r]) for r in range(N)]
    p, k, m = [[gentries(a[r]).astype(np.int64) for r in range(N)] for a in (pg, kg, mg)]
    now = [x[r] for r in range(N)]
    for step in STEP:
        own, land, mosaic = [], [], []
        for r in range(N):
            q = mx_ref.quantize(now[r])
            s = mx_ref.matmul(qu[r], q)
            first = (s[::16] > 0).astype(np.int64)
            e = first + 2 * (s[1::16] > 0).astype(np.int64)
            at = np.zeros((8, C), np.int64)
            for g in range(8):
                power = np.ones(C, np.int64) if g == 0 else e[g - 1][at[g - 1]]
                a = k[r][g]
                for i in range(3): a = np.where(i < power, p[r][g][a], a)
                at[g] = a
            bit = np.take_along_axis(first, at, 1)
            p[r] = np.where(bit != np.take_along_axis(bit, m[r], 1), np.take_along_axis(p[r], m[r], 1), p[r])
            land.append(at)
            own.append(decode(q))
            mosaic.append(mx_ref.quantize(gcols(own[r].astype(BF), at)))
        made = []
        for r in range(N):
            h = [mx_ref.matmul(pick(lay[r], np.arange(128 * b, 128 * b + 128)), mosaic[r ^ step]) * np.float32(0.03125) for b in range(4)]
            made.append(tile([own[r][:, b::4] + gpick(h[b], land[r]) for b in range(4)]))
        now = made
    y, pl = np.zeros((N, 128, C), np.float32), np.zeros((N, 8, 2 * C), np.float32)
    oc, osc = np.zeros((N, 128, 4 * C), np.uint8), np.zeros((N, 16, C), np.uint8)
    for r in range(N):
        q = mx_ref.quantize(now[r])
        y[r] = mx_ref.matmul(mx_ref.quantize(v[r]), q)
        pl[r] = np.concatenate([land[r], p[r]], axis=1)
        oc[r], osc[r] = emit(q)
    return {"y": y, "pl": pl, "oc": oc, "osc": osc}

@@ -1,0 +1,455 @@
+from concourse.bass import DstId, RemoteDMATransfer
+from concourse.mybir import dt, AluOpType, ActivationFunctionType
+
+N = 8
+C = 288
+STEP = [4, 1, 2]
+HALF = C // 2
+ENT = 10
+BLK = 4 * ENT
+BIAS = 144.0
+
+SCRATCH = {
+    "zt": ("sbuf", [128, 4 * C], "bfloat16"), "zq": ("sbuf", [128, C], "float8_e4m3fn_x4"), "zp": ("sbuf", [128, C], "uint8"),
+    "xt": ("sbuf", [128, 4 * C], "bfloat16"), "ut": ("sbuf", [128, 512], "bfloat16"), "vt": ("sbuf", [128, 512], "bfloat16"),
+    "pI": ("sbuf", [128, 18], "int32"), "kI": ("sbuf", [128, 18], "int32"), "mI": ("sbuf", [128, 18], "int32"),
+    "wq": ("sbuf", [128, 512], "float8_e4m3fn_x4"), "wp": ("sbuf", [128, 512], "uint8"),
+    "uq": ("sbuf", [128, 128], "float8_e4m3fn_x4"), "up": ("sbuf", [128, 128], "uint8"),
+    "u3q": ("sbuf", [128, 384], "float8_e4m3fn_x4"), "u3p": ("sbuf", [128, 384], "uint8"),
+    "vq": ("sbuf", [128, 128], "float8_e4m3fn_x4"), "vp": ("sbuf", [128, 128], "uint8"),
+    "ones": ("sbuf", [128, 516], "bfloat16"), "e0": ("sbuf", [128, 516], "bfloat16"),
+    "eq": ("sbuf", [128, 512], "float8_e4m3fn_x4"), "ep": ("sbuf", [128, 512], "uint8"),
+    "ior": ("sbuf", [128, C], "bfloat16"), "idr": ("sbuf", [128, C], "bfloat16"),
+    "pid": ("sbuf", [128, 8], "int32"), "cst": ("sbuf", [128, 32], "float32"),
+    "ulf": ("sbuf", [128, 24], "float32"), "ull": ("sbuf", [128, 24], "uint16"),
+    "m42": ("sbuf", [128, 42], "float32"), "cg": ("sbuf", [128, BLK], "bfloat16"),
+    "pls": ("sbuf", [128, 18], "uint16"), "mls": ("sbuf", [128, 18], "uint16"), "k20": ("sbuf", [128, 20], "uint16"),
+    "kf": ("sbuf", [128, 18], "float32"), "ke": ("sbuf", [128, 20], "float32"), "ko": ("sbuf", [128, 20], "float32"),
+    "tl1": ("sbuf", [128, 20], "uint16"), "tl2": ("sbuf", [128, 20], "uint16"),
+    "xm": ("sbuf", [128, 42], "float32"), "lf": ("sbuf", [128, 20], "float32"),
+    "cP": ("sbuf", [128, 42], "float32"), "cQ": ("sbuf", [128, 42], "float32"), "cR": ("sbuf", [128, 42], "float32"), "cU": ("sbuf", [128, 42], "float32"),
+    "tab": ("sbuf", [128, 8 * BLK], "float32"), "tb6": ("sbuf", [128, 48], "float32"), "tb7": ("sbuf", [128, 48], "float32"), "tf": ("sbuf", [128, 88], "float32"),
+    "w1": ("sbuf", [128, C], "bfloat16"), "w2": ("sbuf", [128, C], "bfloat16"), "wg": ("sbuf", [128, C], "bfloat16"),
+    "s5": ("sbuf", [128, BLK], "float32"), "s5b": ("sbuf", [128, 48], "float32"), "s6": ("sbuf", [128, 88], "float32"),
+    "pm": ("sbuf", [128, 18], "float32"), "l32": ("sbuf", [128, 18], "float32"),
+    "be": ("sbuf", [128, C], "bfloat16"), "be2": ("sbuf", [128, C], "bfloat16"),
+    "ne2": ("sbuf", [128, 2 * C], "bfloat16"), "pd": ("sbuf", [128, 2 * C], "float32"),
+    "m2": ("sbuf", [128, 18], "uint16"), "k20p": ("sbuf", [128, 20], "uint16"),
+    "yo": ("sbuf", [128, C], "float32"), "lo": ("sbuf", [128, C], "float32"), "po": ("sbuf", [128, C], "float32"),
+}
+for _i in range(2):
+    SCRATCH["gg%d" % _i] = ("sbuf", [128, 208], "bfloat16")
+    SCRATCH["gt%d" % _i] = ("sbuf", [128, 352], "bfloat16")
+    SCRATCH["sc%d" % _i] = ("sbuf", [128, BLK], "float32")
+    SCRATCH["of%d" % _i] = ("sbuf", [128, ENT], "uint16")
+for _i in range(4):
+    SCRATCH["tr%d" % _i] = ("sbuf", [128, 368], "bfloat16")
+    SCRATCH["tt%d" % _i] = ("sbuf", [128, 672], "bfloat16")
+    SCRATCH["pr%d" % _i] = ("sbuf", [128, 2 * C], "bfloat16")
+    SCRATCH["q%d" % _i] = ("sbuf", [128, C], "float8_e4m3fn_x4")
+    SCRATCH["qp%d" % _i] = ("sbuf", [128, C], "uint8")
+    SCRATCH["fo%d" % _i] = ("sbuf", [128, C], "bfloat16")
+    SCRATCH["fp%d" % _i] = ("sbuf", [128, C], "bfloat16")
+    SCRATCH["hb%d" % _i] = ("sbuf", [128, C], "float32")
+for _i in range(8):
+    SCRATCH["ps%d" % _i] = ("psum", [128, 512], "float32")
+for _i in range(3):
+    SCRATCH["xn%d" % _i] = ("sbuf", [128, 4 * C], "bfloat16")
+    SCRATCH["aq%d" % _i] = ("sbuf", [128, C], "float8_e4m3fn_x4")
+    SCRATCH["ap%d" % _i] = ("sbuf", [128, C], "uint8")
+    SCRATCH["ll%d" % _i] = ("sbuf", [128, 18], "uint16")
+    SCRATCH["al%d" % _i] = ("sbuf", [128, 18], "uint16")
+
+SEMAPHORES = ["sv", "sa", "st", "sg", "left",
+              "lx", "lu", "lv", "lp", "lk", "lm", "lw", "lws", "out"]
+for _i in range(3):
+    SEMAPHORES += ["rc%d" % _i, "rs%d" % _i, "rL%d" % _i, "aq_%d" % _i, "aL_%d" % _i, "dt%d" % _i]
+
+
+def relays(core, partner, topo):
+    may = [c for c in topo.cores_of(core) if c != core and topo.may_write(c, partner)]
+    same = [c for c in may if topo.die(c) == topo.die(core)]
+    other = [c for c in may if topo.die(c) != topo.die(core)]
+    return [same[0], other[0]], same[1]
+
+
+def bits(es):
+    return sum(1 << e for e in es)
+
+
+def relay_program(g, core, T, topo):
+    home = [c for c in topo.cores_of(core) if T.rank_of(c) is not None]
+    if not home:
+        return
+    home = home[0]
+    left = 0
+    for r in range(3):
+        partner = T.cores[T.rank_of(home) ^ STEP[r]]
+        data, lst = relays(home, partner, topo)
+        rid, pid = topo.addr(partner, core) if core in data or core == lst else (0, 0)
+        es = topo.engines(core, partner)
+        if core in data:
+            k = data.index(core)
+            n_in = len(topo.engines(home, core)) // 2
+            a, b = k * HALF, (k + 1) * HALF
+            g.wait_ge(T.sem["rc%d" % r], n_in)
+            g.remote_dma(T["aq%d" % r][:, a:b].bitcast(dt.uint8), T["aq%d" % r][:, a:b].bitcast(dt.uint8), T.sem["aq_%d" % r], T.sem.left, pid, rid, bits(es))
+            g.wait_ge(T.sem["rs%d" % r], n_in)
+            g.remote_dma(T["ap%d" % r][:, a:b], T["ap%d" % r][:, a:b], T.sem["aq_%d" % r], T.sem.left, pid, rid, bits(es))
+            left += 2 * len(es)
+        if core == lst:
+            g.wait_ge(T.sem["rL%d" % r], len(topo.engines(home, core)))
+            g.remote_dma(T["al%d" % r][:], T["al%d" % r][:], T.sem["aL_%d" % r], T.sem.left, pid, rid, bits(es))
+            left += len(es)
+    if left:
+        g.wait_ge(T.sem.left, left)
+
+
+def rank_program(g, core, T, topo):
+    rank = T.rank_of(core)
+    if rank is None:
+        return relay_program(g, core, T, topo)
+    A = AluOpType
+    F = ActivationFunctionType
+    queue = {"v": g.vector, "a": g.scalar, "t": g.tensor, "g": g, "s": g.sync}
+    own = {"v": "sv", "a": "sa", "t": "st", "g": "sg"}
+    known = {e: {} for e in queue}
+    count, snap, wr, rd = {}, {}, {}, {}
+
+    def need(e, deps):
+        deps = [d for d in set(deps) if known[e].get(d[0], 0) < d[1]]
+        deps.sort(key=lambda d: -sum(snap.get(d, {}).values()))
+        for d in deps:
+            if known[e].get(d[0], 0) >= d[1]:
+                continue
+            queue[e].wait_ge(T.sem[d[0]], d[1])
+            for s, n in list(snap.get(d, {}).items()) + [d]:
+                known[e][s] = max(known[e].get(s, 0), n)
+
+    def before(e, reads, writes):
+        deps = []
+        for k in reads:
+            deps += wr.get(k, [])
+        for k in writes:
+            deps += wr.get(k, []) + rd.get(k, [])
+        need(e, deps)
+
+    def after(reads, writes, d):
+        for k in reads:
+            rd[k] = [x for x in rd.get(k, []) if x[0] != d[0]] + [d]
+        for k in writes:
+            wr[k] = [d]
+            rd[k] = []
+
+    def op(e, reads, writes, call):
+        before(e, reads, writes)
+        s = own[e]
+        count[s] = count.get(s, 0) + 1
+        call().then_inc(T.sem[s], 1)
+        d = (s, count[s])
+        snap[d] = dict(known[e])
+        snap[d][s] = count[s]
+        after(reads, writes, d)
+
+    def dma(e, sem, total, reads, writes, out, in_):
+        before(e, reads, writes)
+        queue[e].dma_start(out, in_).then_inc(T.sem[sem], 16)
+        count[sem] = 16 * total
+        d = (sem, 16 * total)
+        m = snap.setdefault(d, {})
+        for s, n in known[e].items():
+            m[s] = max(m.get(s, 0), n)
+        for k in reads:
+            rd[k] = [x for x in rd.get(k, []) if x != d] + [d]
+        for k in writes:
+            wr[k] = [x for x in wr.get(k, []) if x == d] or [d]
+            rd[k] = []
+
+    def ts(reads, writes, out, in0, s1, op0, s2=None, op1=None):
+        if op1 is None:
+            op("v", reads, writes, lambda: g.vector.tensor_scalar(out, in0, s1, None, op0))
+        else:
+            op("v", reads, writes, lambda: g.vector.tensor_scalar(out, in0, s1, s2, op0, op1))
+
+    def tt(reads, writes, out, in0, in1, o):
+        op("v", reads, writes, lambda: g.vector.tensor_tensor(out, in0, in1, o))
+
+    def cp(reads, writes, out, in_):
+        op("v", reads, writes, lambda: g.vector.tensor_copy(out, in_))
+
+    def act(reads, writes, out, in_, f=F.Copy, **kw):
+        op("a", reads, writes, lambda: g.scalar.activation(out, in_, f, **kw))
+
+    def mm(reads, bank, lhs, lhsp, rhs, rhsp):
+        op("t", reads, ["ps%d" % bank], lambda: g.tensor.matmul_mx(T["ps%d" % bank][:, 0:C], lhs, lhsp, rhs, rhsp, True, True))
+
+    def quant(reads, writes, q, p, t):
+        op("v", reads, writes, lambda: g.vector.quantize_mx(q, p, t))
+
+    def fill(key, ap, c):
+        op("v", [], [key], lambda: g.vector.memset(ap, c))
+
+    dma("s", "lp", 1, [], ["pI"], T.pI[:], T.pg[:])
+    dma("a", "lk", 1, [], ["kI"], T.kI[:], T.kg[:])
+    dma("s", "lx", 1, [], ["xt"], T.xt[:], T.x[:])
+    dma("a", "lu", 1, [], ["ut"], T.ut[:], T.u[:])
+    dma("a", "lm", 1, [], ["mI"], T.mI[:], T.mg[:])
+    dma("s", "lw", 1, [], ["wq"], T.wq[:].bitcast(dt.uint8), T.wc[:])
+    dma("s", "lws", 1, [], ["wp"], T.wp[:], T.ws[:])
+    dma("a", "lv", 1, [], ["vt"], T.vt[:], T.v[:])
+
+    op("g", [], ["pid0"], lambda: g.iota(T.pid[:, 0:1], [[0, 1]], 0, 1))
+    op("g", [], ["ior"], lambda: g.iota(T.ior[:], [[1, C]], -144, 0, allow_small_or_imprecise_dtypes=True))
+    op("g", [], ["ulf"], lambda: g.iota(T.ulf[:, 0:16], [[64, 2], [32, 4], [0, 2]], -96, 0, allow_small_or_imprecise_dtypes=True))
+    op("g", [], ["ulf2"], lambda: g.iota(T.ulf[:, 16:24], [[16, 8]], 0, 0, allow_small_or_imprecise_dtypes=True))
+    fill("ones", T.ones[:], 1.0)
+    op("g", ["ones"], ["e0"], lambda: g.affine_select(T.e0[:], T.ones[:], [[1, 516]], A.is_equal, 0.0, -3, -4))
+    S, I = T.cst, T.pid
+    cc = lambda j: S[:, j:j + 1]
+
+    def plain(key, out, n, c):
+        act(["ones"], [key], out, T.ones[:, 0:n], scale=c)
+
+    fill("ke", T.ke[:], 0.0)
+    fill("ko", T.ko[:], 0.0)
+    plain("pr0", T.pr0[:, 0:2 * C:2], C, 0.0)
+    for i in (1, 2, 3, 0):
+        plain("tr%da" % i, T["tr%d" % i][:, 16:32], 16, 0.0)
+        plain("tr%db" % i, T["tr%d" % i][:, 352:368], 16, 0.0)
+    ts(["pid0"], ["pid1"], I[:, 1:2], I[:, 0:1], 3, A.bitwise_and)
+    ts(["pid0"], ["pid2"], I[:, 2:3], I[:, 0:1], 2, A.logical_shift_right, 3, A.bitwise_and)
+    ts(["pid0"], ["pid3"], I[:, 3:4], I[:, 0:1], 4, A.logical_shift_right, 1, A.bitwise_and)
+    ts(["pid0"], ["pid4"], I[:, 4:5], I[:, 0:1], 5, A.logical_shift_right)
+    ts(["pid3"], ["c3"], cc(3), I[:, 3:4], 0.0, A.is_equal)
+    cp(["pid3"], ["c4"], cc(4), I[:, 3:4])
+    ts(["ior"], ["idr"], T.idr[:], T.ior[:], 0.25, A.mult)
+    cp(["pid1"], ["c0"], cc(0), I[:, 1:2])
+    ts(["pid2"], ["c1"], cc(1), I[:, 2:3], 2.0, A.is_equal)
+    ts(["pid2"], ["c2"], cc(2), I[:, 2:3], 0.0, A.not_equal)
+    ts(["c0", "c1"], ["c7"], cc(7), cc(0), 16.0, A.mult, cc(1), A.add)
+    ts(["ulf", "c7"], ["ull"], T.ull[:, 0:16], T.ulf[:, 0:16], cc(7), A.add, 0.0, A.max)
+    cp(["ulf2"], ["ull2"], T.ull[:, 16:24], T.ulf[:, 16:24])
+    ts(["pid4", "c0"], ["c5"], cc(5), I[:, 4:5], 2.0, A.mult, cc(0), A.add)
+    ts(["c1"], ["c6"], cc(6), cc(1), -2.0, A.mult, 1.0, A.add)
+    for w in range(2):
+        ts(["c5", "c2"], ["c%d" % (8 + w)], cc(8 + w), cc(5), 5.0 - 4 * w, A.not_equal, cc(2), A.mult)
+        ts(["c5", "c6"], ["c%d" % (10 + w)], cc(10 + w), cc(5), 5.0 - 4 * w, A.is_equal, cc(6), A.mult)
+        ts(["c2", "c%d" % (10 + w)], ["c%d" % (12 + w)], cc(12 + w), cc(10 + w), -1e-29, A.add, cc(2), A.mult)
+
+    cp(["pI"], ["pls"], T.pls[:], T.pI[:])
+    cp(["kI"], ["kf"], T.kf[:], T.kI[:])
+    cp(["idr", "pls", "pr0"], ["pr0"], T.pr0[:, 1:2 * C:2], T.idr[:].indirect(T.pls[:]))
+    for h in range(2):
+        for y in range(2):
+            c0 = 10 * (1 - h) + y
+            n = len(range(c0, 18 if h == 0 else 10, 2))
+            m0 = 2 * h + y
+            act(["kf", "c3", "ke"], ["ke%d" % m0], T.ke[:, m0:m0 + 4 * n - 3:4], T.kf[:, c0:c0 + 2 * n - 1:2], scale=cc(3))
+    act(["kf", "c4", "ko"], ["ko1"], T.ko[:, 1:20:2], T.kf[:, 0:10], scale=cc(4))
+    act(["kf", "c4", "ko"], ["ko0"], T.ko[:, 0:15:2], T.kf[:, 10:18], scale=cc(4))
+    tt(["ke0", "ke1", "ke2", "ke3", "ko0", "ko1"], ["ke"], T.ke[:], T.ke[:], T.ko[:], A.add)
+    ts(["ke"], ["k20"], T.k20[:], T.ke[:], 2.0, A.mult, 1.0, A.add)
+    cp(["ke"], ["k20p"], T.k20p[:], T.ke[:])
+    act(["c3", "ones"], ["m42"], T.m42[:, 0:42:2], T.ones[:, 0:21], scale=cc(3))
+    act(["c4", "ones"], ["m42b"], T.m42[:, 1:42:2], T.ones[:, 0:21], scale=cc(4))
+    act(["idr", "k20p"], ["tr0"], T.tr0[:, 32:352], T.idr[:].indirect(T.k20p[:]))
+    plain("tab", T.tab[:], 8 * BLK, 0.0)
+    act(["pr0"], ["pd1"], T.pd[:, 1:2 * C:2], T.pr0[:, 1:2 * C:2])
+    plain("cg0", T.cg[:, 0:BLK:4], ENT, 0.0)
+    plain("cg1", T.cg[:, 1:BLK:4], ENT, 1.0)
+    plain("cg2", T.cg[:, 2:BLK:4], ENT, -1.0)
+    plain("cg3", T.cg[:, 3:BLK:4], ENT, 1.0)
+    plain("c14", cc(14), 1, -1e-29)
+    plain("tb6", T.tb6[:], 48, 0.0)
+    plain("tb7", T.tb7[:], 48, 0.0)
+    for i in range(2):
+        plain("gg%da" % i, T["gg%d" % i][:, 16:32], 16, 0.0)
+        plain("gg%db" % i, T["gg%d" % i][:, 192:208], 16, 0.0)
+    plain("ne0", T.ne2[:, 0:2 * C:2], C, 0.0)
+
+    def turn(n):
+        k, t = "tr%d" % n, "tt%d" % n
+        op("v", [k], [t + "a"], lambda: g.vector.transpose(T[t][:, 0:320], T[k][:, 32:352]))
+        op("v", [k, k + "a", k + "b"], [t + "b"], lambda: g.vector.transpose(T[t][:, 320:672], T[k][:, 16:368]))
+
+    def ent(n):
+        return T["tt%d" % n][:, 0:672:16]
+
+    def aslist(n, name):
+        t = "tt%d" % n
+        tt([t + "a", t + "b", "m42", "m42b"], ["xm"], T.xm[:], ent(n), T.m42[:], A.mult)
+        tt(["xm"], ["lf0"], T.lf[:, 0:20:2], T.xm[:, 0:20:2], T.xm[:, 21:41:2], A.add)
+        tt(["xm"], ["lf1"], T.lf[:, 1:20:2], T.xm[:, 22:42:2], T.xm[:, 1:20:2], A.add)
+        ts(["lf0", "lf1"], [name], T[name][:], T.lf[:], 8.0, A.mult, 2 * BIAS + 1, A.add)
+
+    def rows(n, key, lst, e="v"):
+        (cp if e == "v" else act)([key, lst], ["tr%d" % n], T["tr%d" % n][:, 32:352], T[key][:].indirect(T[lst][:]))
+
+    COMB = [("cR", "cU", A.subtract), ("cP", "cQ", A.subtract), ("cR", "cU", A.add), ("cP", "cQ", A.add)]
+
+    def powers(r):
+        p = "pr%d" % r
+        rows(1, p, "k20")
+        turn(1)
+        aslist(1, "tl1")
+        rows(2, p, "tl1")
+        turn(2)
+        aslist(2, "tl2")
+
+    def tables(r):
+        ks = ["tt1a", "tt1b", "tt2a", "tt2b"]
+        tt(ks, ["cQ"], T.cQ[:], ent(1), ent(2), A.add)
+        tt(ks, ["cU"], T.cU[:], ent(1), ent(2), A.subtract)
+        turn(3)
+        ks = ["tt0a", "tt0b", "tt3a", "tt3b"]
+        tt(ks, ["cP"], T.cP[:], ent(0), ent(3), A.add)
+        tt(ks, ["cR"], T.cR[:], ent(3), ent(0), A.subtract)
+        for h in range(2):
+            for k in range(4):
+                x, y, o = COMB[k]
+                c0 = 6 * BLK + BLK * h + k
+                tt([x, y], ["tab"] if h == k == 0 else ["tab%d" % (4 * h + k)], T.tab[:, c0:c0 + BLK - 3:4], T[x][:, h:20:2], T[y][:, h:20:2], o)
+        ks = ["tab"] + ["tab%d" % i for i in range(1, 8)]
+        for b in range(4):
+            for a in range(b):
+                c0 = 6 * BLK - 2 * BLK * (b - a)
+                dma("s", "dt%d" % r, 6, ks, ["far%d%d" % (a, b)], T.tab[32 * b:32 * b + 32, c0:c0 + 2 * BLK], T.tab[32 * a:32 * a + 32, 6 * BLK:8 * BLK])
+
+    def tails():
+        for k in range(4):
+            x, y, o = COMB[k]
+            tt([x, y, "tb6"], ["tb6_%d" % k], T.tb6[:, 4 + k:4 + k + 41:4], T[x][:, 20:42:2], T[y][:, 20:42:2], o)
+        for k in range(4):
+            x, y, o = COMB[k]
+            tt([x, y, "tb7"], ["tb7_%d" % k], T.tb7[:, k:k + 41:4], T[x][:, 21:42:2], T[y][:, 21:42:2], o)
+        ts(["c4"] + ["tab%d" % i for i in range(4, 8)], ["tfa"], T.tf[:, 0:40], T.tab[:, 7 * BLK:8 * BLK], cc(4), A.mult)
+        ts(["c4", "tb7"] + ["tb7_%d" % k for k in range(4)], ["tfb"], T.tf[:, 40:88], T.tb7[:], cc(4), A.mult)
+
+    powers(0)
+    rows(3, "pr0", "tl2")
+    turn(0)
+    tables(0)
+
+    quant(["xt"], ["q0", "qp0"], T.q0[:], T.qp0[:], T.xt[:])
+    quant(["ut"], ["uq", "up"], T.uq[:], T.up[:], T.ut[:])
+    cp(["uq", "ull", "ull2"], ["u3q"], T.u3q[:].bitcast(dt.uint32), T.uq[:].bitcast(dt.uint32).indirect(T.ull[:]))
+    act(["up", "ull", "ull2"], ["u3p"], T.u3p[:], T.up[:].indirect(T.ull[:]))
+    cp(["mI"], ["mls"], T.mls[:], T.mI[:])
+    ts(["mI"], ["m2"], T.m2[:], T.mI[:], 2.0, A.mult, 1.0, A.add)
+    for b in range(4):
+        quant(["e0"], ["eq%d" % b], T.eq[:, 128 * b:128 * b + 128], T.ep[:, 128 * b:128 * b + 128], T.e0[:, 3 - b:515 - b])
+
+    left = [0]
+    for r in range(3):
+        partner = T.cores[rank ^ STEP[r]]
+        data, lst = relays(core, partner, topo)
+        q, qp, p = "q%d" % r, "qp%d" % r, "pr%d" % r
+        need("g", wr[q])
+        fc, fs = [], []
+        for k, c in enumerate(data):
+            es = topo.engines(core, c)
+            es = es[k * len(es) // 2:(k + 1) * len(es) // 2]
+            rid, pid = topo.addr(c, core)
+            a, b = k * HALF, (k + 1) * HALF
+            fc.append(RemoteDMATransfer(dst_ids=[DstId(rid=rid, pnc=pid)], dma_engine_mask=bits(es), remote_sem=T.sem["rc%d" % r],
+                                        src=T[q][:, a:b].bitcast(dt.uint8), dst=T["aq%d" % r][:, a:b].bitcast(dt.uint8)))
+            fs.append(RemoteDMATransfer(dst_ids=[DstId(rid=rid, pnc=pid)], dma_engine_mask=bits(es), remote_sem=T.sem["rs%d" % r],
+                                        src=T[qp][:, a:b], dst=T["ap%d" % r][:, a:b]))
+            left[0] += 2 * len(es)
+        g.remote_dma_fused(fc, local_sem=T.sem.left)
+        g.remote_dma_fused(fs, local_sem=T.sem.left)
+        for w in range(3):
+            mm([q, qp, "u3q", "u3p"], w, T.u3q[:, 128 * w:128 * w + 128], T.u3p[:, 128 * w:128 * w + 128], T[q][:], T[qp][:])
+        for w in range(2):
+            act(["ps%d" % w, "c%d" % (8 + w), "c%d" % (12 + w)], ["w%d" % (w + 1)], T["w%d" % (w + 1)][:], T["ps%d" % w][:, 0:C], F.Sign, scale=cc(8 + w), bias=cc(12 + w))
+        act(["ps2", "c14"], ["wg"], T.wg[:], T.ps2[:, 0:C], F.Sign, bias=cc(14))
+        for b in range(4):
+            mm([q, qp, "eq%d" % b], 3 + b, T.eq[:, 128 * b:128 * b + 128], T.ep[:, 128 * b:128 * b + 128], T[q][:], T[qp][:])
+        for b in range(4):
+            act(["ps%d" % (3 + b)], ["fo%d" % b], T["fo%d" % b][:], T["ps%d" % (3 + b)][:, 0:C])
+        tails()
+        tt([p, "pd1", "m2"], ["pd0"], T.pd[:, 0:2 * C:2], T[p][:].indirect(T.m2[:]), T.pd[:, 1:2 * C:2], A.subtract)
+        far = ["far%d%d" % (a, b) for b in range(4) for a in range(b)]
+        scan = lambda out, d0, d1: (lambda: g.vector.tensor_tensor_scan(out, d0, d1, 0.0, A.mult, A.add))
+        op("v", ["cg0", "cg1", "cg2", "cg3", "tab"] + far, ["sc0"], scan(T.sc0[:], T.cg[:], T.tab[:, 0:BLK]))
+        ts(["sc0"], ["of0"], T.of0[:], T.sc0[:, 3:BLK:4], BIAS, A.add)
+        for t in range(7):
+            i, j = t % 2, (t + 1) % 2
+            w, lane = "w%d" % (1 + t // 4), t % 4
+            gg, gt = "gg%d" % i, "gt%d" % i
+            cp([w, "of%d" % i], [gg], T[gg][:, 32:192], T[w][:].indirect(T["of%d" % i][:]))
+            op("v", [gg], [gt], lambda: g.vector.transpose(T[gt][:, 0:160], T[gg][:, 32:192]))
+            d1 = ["tab%d" % k for k in range(8)] + ["tab"] + far
+            if t < 5:
+                op("v", [gt] + d1, ["sc%d" % j], scan(T["sc%d" % j][:], T[gt][:, lane:160:4], T.tab[:, BLK * (t + 1):BLK * (t + 2)]))
+                ts(["sc%d" % j], ["of%d" % j], T["of%d" % j][:], T["sc%d" % j][:, 3:BLK:4], BIAS, A.add)
+            elif t == 5:
+                op("v", [gt] + d1, ["s5"], scan(T.s5[:], T[gt][:, lane:160:4], T.tab[:, 6 * BLK:7 * BLK]))
+                op("v", [gg, gg + "a", gg + "b"], [gt + "b"], lambda: g.vector.transpose(T[gt][:, 160:352], T[gg][:, 16:208]))
+                ts(["s5"], ["of0"], T.of0[:], T.s5[:, 3:BLK:4], BIAS, A.add)
+                op("v", [gt + "b", "tb6"] + ["tb6_%d" % k for k in range(4)], ["s5b"], scan(T.s5b[:], T[gt][:, 160 + lane:352:4], T.tb6[:]))
+                act(["s5", "c3"], ["pm0"], T.pm[:, 0:10:2], T.s5[:, 7:40:8], scale=cc(3))
+                act(["s5", "c3"], ["pm1"], T.pm[:, 10:18:2], T.s5[:, 3:32:8], scale=cc(3))
+                act(["s5b", "c3"], ["pm2"], T.pm[:, 1:10:2], T.s5b[:, 15:48:8], scale=cc(3))
+                act(["s5b", "c3"], ["pm3"], T.pm[:, 11:18:2], T.s5b[:, 11:36:8], scale=cc(3))
+            else:
+                op("v", [gg, gg + "a", gg + "b"], [gt + "b"], lambda: g.vector.transpose(T[gt][:, 160:352], T[gg][:, 16:208]))
+                op("v", [gt, gt + "b", "tfa", "tfb"], ["s6"], scan(T.s6[:], T[gt][:, lane:352:4], T.tf[:]))
+        ll = "ll%d" % r
+        tt(["s6", "pm0", "pm1", "pm2", "pm3"], ["l32"], T.l32[:], T.s6[:, 3:72:4], T.pm[:], A.add)
+        ts(["l32"], [ll], T[ll][:], T.l32[:], BIAS, A.add)
+        need("g", wr[ll])
+        rid, pid = topo.addr(lst, core)
+        es = topo.engines(core, lst)
+        g.remote_dma(T["al%d" % r][:], T[ll][:], T.sem["rL%d" % r], T.sem.left, pid, rid, bits(es))
+        left[0] += len(es)
+        np_ = "pr%d" % (r + 1)
+        act(["wg", ll], ["be2"], T.be2[:], T.wg[:].indirect(T[ll][:]))
+        cp(["wg", ll], ["be"], T.be[:], T.wg[:].indirect(T[ll][:]))
+        tt(["be", "be2", "mls"], ["ne1"], T.ne2[:, 1:2 * C:2], T.be[:].indirect(T.mls[:]), T.be2[:], A.not_equal)
+        op("v", ["ne0", "ne1", "pd0", "pd1"], [np_], scan(T[np_][:], T.ne2[:], T.pd[:]))
+        if r < 2:
+            powers(r + 1)
+        else:
+            cp(["idr", ll], ["lo"], T.lo[:], T.idr[:].indirect(T[ll][:]))
+            quant(["vt"], ["vq"], T.vq[:], T.vp[:], T.vt[:])
+            ts(["lo"], ["lo"], T.lo[:], T.lo[:], 4.0, A.mult, BIAS, A.add)
+            ts([np_], ["po"], T.po[:], T[np_][:, 1:2 * C:2], 4.0, A.mult, BIAS, A.add)
+            dma("s", "out", 8, ["lo"], ["pl0"], T.pl[:, 0:C], T.lo[0:128:16, :])
+            dma("s", "out", 8, ["po"], ["pl1"], T.pl[:, C:2 * C], T.po[0:128:16, :])
+        wr["aq"] = [("aq_%d" % r, sum(2 * len(topo.engines(c, core)) for c in relays(partner, core, topo)[0]))]
+        wr["al"] = [("aL_%d" % r, len(topo.engines(relays(partner, core, topo)[1], core)))]
+        count["aq_%d" % r], count["aL_%d" % r] = wr["aq"][0][1], wr["al"][0][1]
+        for b in range(4):
+            mm(["aq", "eq%d" % b], (7 + b) % 8, T.eq[:, 128 * b:128 * b + 128], T.ep[:, 128 * b:128 * b + 128], T["aq%d" % r][:], T["ap%d" % r][:])
+        for b in range(4):
+            act(["ps%d" % ((7 + b) % 8)], ["fp%d" % b], T["fp%d" % b][:], T["ps%d" % ((7 + b) % 8)][:, 0:C])
+        al, zt = T["al%d" % r], T.zt
+        for b in (0, 2, 1, 3):
+            if b < 2:
+                cp(["fp%d" % b, "al"], ["zt%d" % b], zt[:, b:4 * C:4], T["fp%d" % b][:].indirect(al[:]))
+            else:
+                act(["fp%d" % b, "al"], ["zt%d" % b], zt[:, b:4 * C:4], T["fp%d" % b][:].indirect(al[:]))
+        quant(["zt%d" % b for b in range(4)], ["zq"], T.zq[:], T.zp[:], zt[:])
+        if r < 2:
+            rows(3, np_, "tl2", "a")
+            tables(r + 1)
+        for b in range(4):
+            mm(["zq", "wq", "wp"], 3 + b, T.wq[:, 128 * b:128 * b + 128], T.wp[:, 128 * b:128 * b + 128], T.zq[:], T.zp[:])
+        xn = T["xn%d" % r]
+        for b in range(4):
+            act(["ps%d" % (3 + b)], ["hb%d" % b], T["hb%d" % b][:], T["ps%d" % (3 + b)][:, 0:C], scale=0.03125)
+            tt(["hb%d" % b, "fo%d" % b, ll], ["xn%d" % b], xn[:, b:4 * C:4], T["hb%d" % b][:].indirect(T[ll][:]), T["fo%d" % b][:], A.add)
+        if r < 2:
+            act([np_], ["pd1"], T.pd[:, 1:2 * C:2], T[np_][:, 1:2 * C:2])
+        nq, nqp = "q%d" % (r + 1), "qp%d" % (r + 1)
+        quant(["xn%d" % b for b in range(4)], [nq, nqp], T[nq][:], T[nqp][:], xn[:])
+    mm(["q3", "qp3", "vq"], 7, T.vq[:], T.vp[:], T.q3[:], T.qp3[:])
+    dma("s", "out", 8, ["q3"], ["oc"], T.oc[:], T.q3[:].bitcast(dt.uint8))
+    for k in range(4):
+        dma("s" if k % 2 else "a", "out", 8, ["qp3"], ["osc%d" % k], T.osc[4 * k:4 * k + 4, :], T.qp3[32 * k:32 * k + 4, :])
+    act(["ps7"], ["yo"], T.yo[:], T.ps7[:, 0:C])
+    dma("s", "out", 8, ["yo"], ["y"], T.y[:], T.yo[:])
+    g.wait_ge(T.sem.left, left[0])
+    for s in sorted(count):
+        g.wait_ge(T.sem[s], count[s])

@@ -70,7 +70,7 @@ def relays(core, partner, topo):
     may = [c for c in topo.cores_of(core) if c != core and topo.may_write(c, partner)]
     same = [c for c in may if topo.die(c) == topo.die(core)]
     other = [c for c in may if topo.die(c) != topo.die(core)]
-    return [same[0], other[0]], same[1]
+    return [same[0], other[0]], same[0]
 
 
 def bits(es):
@@ -225,19 +225,13 @@ def rank_program(g, core, T, topo):
     ts(["ior"], ["idr"], T.idr[:], T.ior[:], 0.25, A.mult)
     cp(["pid1"], ["c0"], cc(0), I[:, 1:2])
     ts(["pid2"], ["c1"], cc(1), I[:, 2:3], 2.0, A.is_equal)
-    ts(["pid2"], ["c2"], cc(2), I[:, 2:3], 0.0, A.not_equal)
     ts(["c0", "c1"], ["c7"], cc(7), cc(0), 16.0, A.mult, cc(1), A.add)
     ts(["ulf", "c7"], ["ull"], T.ull[:, 0:16], T.ulf[:, 0:16], cc(7), A.add, 0.0, A.max)
     cp(["ulf2"], ["ull2"], T.ull[:, 16:24], T.ulf[:, 16:24])
-    ts(["pid4", "c0"], ["c5"], cc(5), I[:, 4:5], 2.0, A.mult, cc(0), A.add)
-    ts(["c1"], ["c6"], cc(6), cc(1), -2.0, A.mult, 1.0, A.add)
-    for w in range(2):
-        ts(["c5", "c2"], ["c%d" % (8 + w)], cc(8 + w), cc(5), 5.0 - 4 * w, A.not_equal, cc(2), A.mult)
-        ts(["c5", "c6"], ["c%d" % (10 + w)], cc(10 + w), cc(5), 5.0 - 4 * w, A.is_equal, cc(6), A.mult)
-        ts(["c2", "c%d" % (10 + w)], ["c%d" % (12 + w)], cc(12 + w), cc(10 + w), -1e-29, A.add, cc(2), A.mult)
 
-    cp(["pI"], ["pls"], T.pls[:], T.pI[:])
     cp(["kI"], ["kf"], T.kf[:], T.kI[:])
+    cp(["pI"], ["pls"], T.pls[:], T.pI[:])
+    ts(["pI"], ["tl1"], T.tl1[:, 0:18], T.pI[:], 2.0, A.mult, 1.0, A.add)
     cp(["idr", "pls", "pr0"], ["pr0"], T.pr0[:, 1:2 * C:2], T.idr[:].indirect(T.pls[:]))
     for h in range(2):
         for y in range(2):
@@ -250,10 +244,13 @@ def rank_program(g, core, T, topo):
     tt(["ke0", "ke1", "ke2", "ke3", "ko0", "ko1"], ["ke"], T.ke[:], T.ke[:], T.ko[:], A.add)
     ts(["ke"], ["k20"], T.k20[:], T.ke[:], 2.0, A.mult, 1.0, A.add)
     cp(["ke"], ["k20p"], T.k20p[:], T.ke[:])
-    act(["c3", "ones"], ["m42"], T.m42[:, 0:42:2], T.ones[:, 0:21], scale=cc(3))
-    act(["c4", "ones"], ["m42b"], T.m42[:, 1:42:2], T.ones[:, 0:21], scale=cc(4))
+    cp(["pr0", "tl1"], ["pr1"], T.pr1[:, 0:C], T.pr0[:].indirect(T.tl1[:, 0:18]))
+    act(["pr0", "k20"], ["tr1"], T.tr1[:, 32:352], T.pr0[:].indirect(T.k20[:]))
+    act(["pr1", "k20p"], ["tr2"], T.tr2[:, 32:352], T.pr1[:, 0:C].indirect(T.k20p[:]))
     act(["idr", "k20p"], ["tr0"], T.tr0[:, 32:352], T.idr[:].indirect(T.k20p[:]))
     plain("tab", T.tab[:], 8 * BLK, 0.0)
+    act(["c3", "ones"], ["m42"], T.m42[:, 0:42:2], T.ones[:, 0:21], scale=cc(3))
+    act(["c4", "ones"], ["m42b"], T.m42[:, 1:42:2], T.ones[:, 0:21], scale=cc(4))
     act(["pr0"], ["pd1"], T.pd[:, 1:2 * C:2], T.pr0[:, 1:2 * C:2])
     plain("cg0", T.cg[:, 0:BLK:4], ENT, 0.0)
     plain("cg1", T.cg[:, 1:BLK:4], ENT, 1.0)
@@ -278,9 +275,8 @@ def rank_program(g, core, T, topo):
     def aslist(n, name):
         t = "tt%d" % n
         tt([t + "a", t + "b", "m42", "m42b"], ["xm"], T.xm[:], ent(n), T.m42[:], A.mult)
-        tt(["xm"], ["lf0"], T.lf[:, 0:20:2], T.xm[:, 0:20:2], T.xm[:, 21:41:2], A.add)
-        tt(["xm"], ["lf1"], T.lf[:, 1:20:2], T.xm[:, 22:42:2], T.xm[:, 1:20:2], A.add)
-        ts(["lf0", "lf1"], [name], T[name][:], T.lf[:], 8.0, A.mult, 2 * BIAS + 1, A.add)
+        tt(["xm"], ["lf"], T.lf[:], T.xm[:, 0:20], T.xm[:, 21:41], A.add)
+        ts(["lf"], [name], T[name][:], T.lf[:], 8.0, A.mult, 2 * BIAS + 1, A.add)
 
     def rows(n, key, lst, e="v"):
         (cp if e == "v" else act)([key, lst], ["tr%d" % n], T["tr%d" % n][:, 32:352], T[key][:].indirect(T[lst][:]))
@@ -295,11 +291,14 @@ def rank_program(g, core, T, topo):
         rows(2, p, "tl1")
         turn(2)
         aslist(2, "tl2")
+        middle()
 
-    def tables(r):
+    def middle():
         ks = ["tt1a", "tt1b", "tt2a", "tt2b"]
         tt(ks, ["cQ"], T.cQ[:], ent(1), ent(2), A.add)
         tt(ks, ["cU"], T.cU[:], ent(1), ent(2), A.subtract)
+
+    def tables(r):
         turn(3)
         ks = ["tt0a", "tt0b", "tt3a", "tt3b"]
         tt(ks, ["cP"], T.cP[:], ent(0), ent(3), A.add)
@@ -315,18 +314,23 @@ def rank_program(g, core, T, topo):
                 c0 = 6 * BLK - 2 * BLK * (b - a)
                 dma("s", "dt%d" % r, 6, ks, ["far%d%d" % (a, b)], T.tab[32 * b:32 * b + 32, c0:c0 + 2 * BLK], T.tab[32 * a:32 * a + 32, 6 * BLK:8 * BLK])
 
-    def tails():
-        for k in range(4):
-            x, y, o = COMB[k]
+    def tail(i):
+        k = i % 4
+        x, y, o = COMB[k]
+        if i < 4:
             tt([x, y, "tb6"], ["tb6_%d" % k], T.tb6[:, 4 + k:4 + k + 41:4], T[x][:, 20:42:2], T[y][:, 20:42:2], o)
-        for k in range(4):
-            x, y, o = COMB[k]
+        else:
             tt([x, y, "tb7"], ["tb7_%d" % k], T.tb7[:, k:k + 41:4], T[x][:, 21:42:2], T[y][:, 21:42:2], o)
-        ts(["c4"] + ["tab%d" % i for i in range(4, 8)], ["tfa"], T.tf[:, 0:40], T.tab[:, 7 * BLK:8 * BLK], cc(4), A.mult)
-        ts(["c4", "tb7"] + ["tb7_%d" % k for k in range(4)], ["tfb"], T.tf[:, 40:88], T.tb7[:], cc(4), A.mult)
 
-    powers(0)
-    rows(3, "pr0", "tl2")
+    def ends():
+        act(["c4"] + ["tab%d" % i for i in range(4, 8)], ["tfa"], T.tf[:, 0:40], T.tab[:, 7 * BLK:8 * BLK], scale=cc(4))
+        act(["c4", "tb7"] + ["tb7_%d" % k for k in range(4)], ["tfb"], T.tf[:, 40:88], T.tb7[:], scale=cc(4))
+
+    cp(["pr1", "pls"], ["pr2"], T.pr2[:, 0:C], T.pr1[:, 0:C].indirect(T.pls[:]))
+    cp(["pr2", "k20p"], ["tr3"], T.tr3[:, 32:352], T.pr2[:, 0:C].indirect(T.k20p[:]))
+    turn(1)
+    turn(2)
+    middle()
     turn(0)
     tables(0)
 
@@ -334,10 +338,21 @@ def rank_program(g, core, T, topo):
     quant(["ut"], ["uq", "up"], T.uq[:], T.up[:], T.ut[:])
     cp(["uq", "ull", "ull2"], ["u3q"], T.u3q[:].bitcast(dt.uint32), T.uq[:].bitcast(dt.uint32).indirect(T.ull[:]))
     act(["up", "ull", "ull2"], ["u3p"], T.u3p[:], T.up[:].indirect(T.ull[:]))
+    ts(["pid2"], ["c2"], cc(2), I[:, 2:3], 0.0, A.not_equal)
+    ts(["pid4", "c0"], ["c5"], cc(5), I[:, 4:5], 2.0, A.mult, cc(0), A.add)
+    ts(["c1"], ["c6"], cc(6), cc(1), -2.0, A.mult, 1.0, A.add)
+    for w in range(2):
+        ts(["c5", "c2"], ["c%d" % (8 + w)], cc(8 + w), cc(5), 5.0 - 4 * w, A.not_equal, cc(2), A.mult)
+        ts(["c5", "c6"], ["c%d" % (10 + w)], cc(10 + w), cc(5), 5.0 - 4 * w, A.is_equal, cc(6), A.mult)
+        ts(["c2", "c%d" % (10 + w)], ["c%d" % (12 + w)], cc(12 + w), cc(10 + w), -1e-29, A.add, cc(2), A.mult)
     cp(["mI"], ["mls"], T.mls[:], T.mI[:])
     ts(["mI"], ["m2"], T.m2[:], T.mI[:], 2.0, A.mult, 1.0, A.add)
-    for b in range(4):
+
+    def unit(b):
         quant(["e0"], ["eq%d" % b], T.eq[:, 128 * b:128 * b + 128], T.ep[:, 128 * b:128 * b + 128], T.e0[:, 3 - b:515 - b])
+
+    unit(0)
+    unit(1)
 
     left = [0]
     for r in range(3):
@@ -360,15 +375,33 @@ def rank_program(g, core, T, topo):
         g.remote_dma_fused(fs, local_sem=T.sem.left)
         for w in range(3):
             mm([q, qp, "u3q", "u3p"], w, T.u3q[:, 128 * w:128 * w + 128], T.u3p[:, 128 * w:128 * w + 128], T[q][:], T[qp][:])
-        for w in range(2):
-            act(["ps%d" % w, "c%d" % (8 + w), "c%d" % (12 + w)], ["w%d" % (w + 1)], T["w%d" % (w + 1)][:], T["ps%d" % w][:, 0:C], F.Sign, scale=cc(8 + w), bias=cc(12 + w))
-        act(["ps2", "c14"], ["wg"], T.wg[:], T.ps2[:, 0:C], F.Sign, bias=cc(14))
-        for b in range(4):
+
+        def own_f(b):
             mm([q, qp, "eq%d" % b], 3 + b, T.eq[:, 128 * b:128 * b + 128], T.ep[:, 128 * b:128 * b + 128], T[q][:], T[qp][:])
-        for b in range(4):
-            act(["ps%d" % (3 + b)], ["fo%d" % b], T["fo%d" % b][:], T["ps%d" % (3 + b)][:, 0:C])
-        tails()
-        tt([p, "pd1", "m2"], ["pd0"], T.pd[:, 0:2 * C:2], T[p][:].indirect(T.m2[:]), T.pd[:, 1:2 * C:2], A.subtract)
+
+        for b in range(4 if r else 2):
+            own_f(b)
+
+        def signs(w):
+            act(["ps%d" % w, "c%d" % (8 + w), "c%d" % (12 + w)], ["w%d" % (w + 1)], T["w%d" % (w + 1)][:], T["ps%d" % w][:, 0:C], F.Sign, scale=cc(8 + w), bias=cc(12 + w))
+
+        def meanwhile(t):
+            if t == 0:
+                signs(1)
+            elif t == 1:
+                act(["ps2", "c14"], ["wg"], T.wg[:], T.ps2[:, 0:C], F.Sign, bias=cc(14))
+            elif t in (2, 3, 7, 8):
+                b = (2, 3, 7, 8).index(t)
+                act(["ps%d" % (3 + b)], ["fo%d" % b], T["fo%d" % b][:], T["ps%d" % (3 + b)][:, 0:C])
+            elif t == 4:
+                ends()
+
+        signs(0)
+        def differ():
+            tt([p, "pd1", "m2"], ["pd0"], T.pd[:, 0:2 * C:2], T[p][:].indirect(T.m2[:]), T.pd[:, 1:2 * C:2], A.subtract)
+
+        if r:
+            differ()
         far = ["far%d%d" % (a, b) for b in range(4) for a in range(b)]
         scan = lambda out, d0, d1: (lambda: g.vector.tensor_tensor_scan(out, d0, d1, 0.0, A.mult, A.add))
         op("v", ["cg0", "cg1", "cg2", "cg3", "tab"] + far, ["sc0"], scan(T.sc0[:], T.cg[:], T.tab[:, 0:BLK]))
@@ -377,23 +410,32 @@ def rank_program(g, core, T, topo):
             i, j = t % 2, (t + 1) % 2
             w, lane = "w%d" % (1 + t // 4), t % 4
             gg, gt = "gg%d" % i, "gt%d" % i
-            cp([w, "of%d" % i], [gg], T[gg][:, 32:192], T[w][:].indirect(T["of%d" % i][:]))
-            op("v", [gg], [gt], lambda: g.vector.transpose(T[gt][:, 0:160], T[gg][:, 32:192]))
+            cp([w, "of%d" % i], [gg], T[gg][:, 32:128], T[w][:].indirect(T["of%d" % i][:, 0:6]))
+            act([w, "of%d" % i], [gg + "s"], T[gg][:, 128:192], T[w][:].indirect(T["of%d" % i][:, 6:10]))
+            if t < 4:
+                tail(2 * t)
+            op("v", [gg, gg + "s"], [gt], lambda: g.vector.transpose(T[gt][:, 0:160], T[gg][:, 32:192]))
+            if t < 4:
+                tail(2 * t + 1)
+            elif r == 0 and t < 6:
+                unit(t - 2)
+                own_f(t - 2)
+            meanwhile(t)
             d1 = ["tab%d" % k for k in range(8)] + ["tab"] + far
             if t < 5:
                 op("v", [gt] + d1, ["sc%d" % j], scan(T["sc%d" % j][:], T[gt][:, lane:160:4], T.tab[:, BLK * (t + 1):BLK * (t + 2)]))
                 ts(["sc%d" % j], ["of%d" % j], T["of%d" % j][:], T["sc%d" % j][:, 3:BLK:4], BIAS, A.add)
             elif t == 5:
                 op("v", [gt] + d1, ["s5"], scan(T.s5[:], T[gt][:, lane:160:4], T.tab[:, 6 * BLK:7 * BLK]))
-                op("v", [gg, gg + "a", gg + "b"], [gt + "b"], lambda: g.vector.transpose(T[gt][:, 160:352], T[gg][:, 16:208]))
+                op("v", [gg, gg + "s", gg + "a", gg + "b"], [gt + "b"], lambda: g.vector.transpose(T[gt][:, 160:352], T[gg][:, 16:208]))
                 ts(["s5"], ["of0"], T.of0[:], T.s5[:, 3:BLK:4], BIAS, A.add)
                 op("v", [gt + "b", "tb6"] + ["tb6_%d" % k for k in range(4)], ["s5b"], scan(T.s5b[:], T[gt][:, 160 + lane:352:4], T.tb6[:]))
+            else:
                 act(["s5", "c3"], ["pm0"], T.pm[:, 0:10:2], T.s5[:, 7:40:8], scale=cc(3))
                 act(["s5", "c3"], ["pm1"], T.pm[:, 10:18:2], T.s5[:, 3:32:8], scale=cc(3))
                 act(["s5b", "c3"], ["pm2"], T.pm[:, 1:10:2], T.s5b[:, 15:48:8], scale=cc(3))
                 act(["s5b", "c3"], ["pm3"], T.pm[:, 11:18:2], T.s5b[:, 11:36:8], scale=cc(3))
-            else:
-                op("v", [gg, gg + "a", gg + "b"], [gt + "b"], lambda: g.vector.transpose(T[gt][:, 160:352], T[gg][:, 16:208]))
+                op("v", [gg, gg + "s", gg + "a", gg + "b"], [gt + "b"], lambda: g.vector.transpose(T[gt][:, 160:352], T[gg][:, 16:208]))
                 op("v", [gt, gt + "b", "tfa", "tfb"], ["s6"], scan(T.s6[:], T[gt][:, lane:352:4], T.tf[:]))
         ll = "ll%d" % r
         tt(["s6", "pm0", "pm1", "pm2", "pm3"], ["l32"], T.l32[:], T.s6[:, 3:72:4], T.pm[:], A.add)
@@ -405,7 +447,11 @@ def rank_program(g, core, T, topo):
         left[0] += len(es)
         np_ = "pr%d" % (r + 1)
         act(["wg", ll], ["be2"], T.be2[:], T.wg[:].indirect(T[ll][:]))
+        meanwhile(7)
+        meanwhile(8)
         cp(["wg", ll], ["be"], T.be[:], T.wg[:].indirect(T[ll][:]))
+        if r == 0:
+            differ()
         tt(["be", "be2", "mls"], ["ne1"], T.ne2[:, 1:2 * C:2], T.be[:].indirect(T.mls[:]), T.be2[:], A.not_equal)
         op("v", ["ne0", "ne1", "pd0", "pd1"], [np_], scan(T[np_][:], T.ne2[:], T.pd[:]))
         if r < 2:

from concourse.bass import DstId, RemoteDMATransfer
from concourse.mybir import dt, AluOpType, ActivationFunctionType

N = 8
C = 288
STEP = [4, 1, 2]
HALF = C // 2
ENT = 10
BLK = 4 * ENT
BIAS = 144.0

SCRATCH = {
    "zt": ("sbuf", [128, 4 * C], "bfloat16"), "zq": ("sbuf", [128, C], "float8_e4m3fn_x4"), "zp": ("sbuf", [128, C], "uint8"),
    "xt": ("sbuf", [128, 4 * C], "bfloat16"), "ut": ("sbuf", [128, 512], "bfloat16"), "vt": ("sbuf", [128, 512], "bfloat16"),
    "pI": ("sbuf", [128, 18], "int32"), "kI": ("sbuf", [128, 18], "int32"), "mI": ("sbuf", [128, 18], "int32"),
    "wq": ("sbuf", [128, 512], "float8_e4m3fn_x4"), "wp": ("sbuf", [128, 512], "uint8"),
    "uq": ("sbuf", [128, 128], "float8_e4m3fn_x4"), "up": ("sbuf", [128, 128], "uint8"),
    "u3q": ("sbuf", [128, 384], "float8_e4m3fn_x4"), "u3p": ("sbuf", [128, 384], "uint8"),
    "vq": ("sbuf", [128, 128], "float8_e4m3fn_x4"), "vp": ("sbuf", [128, 128], "uint8"),
    "ones": ("sbuf", [128, 516], "bfloat16"), "e0": ("sbuf", [128, 516], "bfloat16"),
    "eq": ("sbuf", [128, 512], "float8_e4m3fn_x4"), "ep": ("sbuf", [128, 512], "uint8"),
    "ior": ("sbuf", [128, C], "bfloat16"), "idr": ("sbuf", [128, C], "bfloat16"),
    "pid": ("sbuf", [128, 8], "int32"), "cst": ("sbuf", [128, 32], "float32"),
    "ulf": ("sbuf", [128, 24], "float32"), "ull": ("sbuf", [128, 24], "uint16"),
    "m42": ("sbuf", [128, 42], "float32"), "cg": ("sbuf", [128, BLK], "bfloat16"),
    "pls": ("sbuf", [128, 18], "uint16"), "mls": ("sbuf", [128, 18], "uint16"), "k20": ("sbuf", [128, 20], "uint16"),
    "kf": ("sbuf", [128, 18], "float32"), "ke": ("sbuf", [128, 20], "float32"), "ko": ("sbuf", [128, 20], "float32"),
    "tl1": ("sbuf", [128, 20], "uint16"), "tl2": ("sbuf", [128, 20], "uint16"),
    "xm": ("sbuf", [128, 42], "float32"), "lf": ("sbuf", [128, 20], "float32"),
    "cP": ("sbuf", [128, 42], "float32"), "cQ": ("sbuf", [128, 42], "float32"), "cR": ("sbuf", [128, 42], "float32"), "cU": ("sbuf", [128, 42], "float32"),
    "tab": ("sbuf", [128, 8 * BLK], "float32"), "tb6": ("sbuf", [128, 48], "float32"), "tb7": ("sbuf", [128, 48], "float32"), "tf": ("sbuf", [128, 88], "float32"),
    "w1": ("sbuf", [128, C], "bfloat16"), "w2": ("sbuf", [128, C], "bfloat16"), "wg": ("sbuf", [128, C], "bfloat16"),
    "s5": ("sbuf", [128, BLK], "float32"), "s5b": ("sbuf", [128, 48], "float32"), "s6": ("sbuf", [128, 88], "float32"),
    "pm": ("sbuf", [128, 18], "float32"), "l32": ("sbuf", [128, 18], "float32"),
    "be": ("sbuf", [128, C], "bfloat16"), "be2": ("sbuf", [128, C], "bfloat16"),
    "ne2": ("sbuf", [128, 2 * C], "bfloat16"), "pd": ("sbuf", [128, 2 * C], "float32"),
    "m2": ("sbuf", [128, 18], "uint16"), "k20p": ("sbuf", [128, 20], "uint16"),
    "yo": ("sbuf", [128, C], "float32"), "lo": ("sbuf", [128, C], "float32"), "po": ("sbuf", [128, C], "float32"),
}
for _i in range(2):
    SCRATCH["gg%d" % _i] = ("sbuf", [128, 208], "bfloat16")
    SCRATCH["gt%d" % _i] = ("sbuf", [128, 352], "bfloat16")
    SCRATCH["sc%d" % _i] = ("sbuf", [128, BLK], "float32")
    SCRATCH["of%d" % _i] = ("sbuf", [128, ENT], "uint16")
for _i in range(4):
    SCRATCH["tr%d" % _i] = ("sbuf", [128, 368], "bfloat16")
    SCRATCH["tt%d" % _i] = ("sbuf", [128, 672], "bfloat16")
    SCRATCH["pr%d" % _i] = ("sbuf", [128, 2 * C], "bfloat16")
    SCRATCH["q%d" % _i] = ("sbuf", [128, C], "float8_e4m3fn_x4")
    SCRATCH["qp%d" % _i] = ("sbuf", [128, C], "uint8")
    SCRATCH["fo%d" % _i] = ("sbuf", [128, C], "bfloat16")
    SCRATCH["fp%d" % _i] = ("sbuf", [128, C], "bfloat16")
    SCRATCH["hb%d" % _i] = ("sbuf", [128, C], "float32")
for _i in range(8):
    SCRATCH["ps%d" % _i] = ("psum", [128, 512], "float32")
for _i in range(3):
    SCRATCH["xn%d" % _i] = ("sbuf", [128, 4 * C], "bfloat16")
    SCRATCH["aq%d" % _i] = ("sbuf", [128, C], "float8_e4m3fn_x4")
    SCRATCH["ap%d" % _i] = ("sbuf", [128, C], "uint8")
    SCRATCH["ll%d" % _i] = ("sbuf", [128, 18], "uint16")
    SCRATCH["al%d" % _i] = ("sbuf", [128, 18], "uint16")

SEMAPHORES = ["sv", "sa", "st", "sg", "left",
              "lx", "lu", "lv", "lp", "lk", "lm", "lw", "lws", "out"]
for _i in range(3):
    SEMAPHORES += ["rc%d" % _i, "rs%d" % _i, "rL%d" % _i, "aq_%d" % _i, "aL_%d" % _i, "dt%d" % _i]


def relays(core, partner, topo):
    may = [c for c in topo.cores_of(core) if c != core and topo.may_write(c, partner)]
    same = [c for c in may if topo.die(c) == topo.die(core)]
    other = [c for c in may if topo.die(c) != topo.die(core)]
    return [same[0], other[0]], same[0]


def bits(es):
    return sum(1 << e for e in es)


def relay_program(g, core, T, topo):
    home = [c for c in topo.cores_of(core) if T.rank_of(c) is not None]
    if not home:
        return
    home = home[0]
    left = 0
    for r in range(3):
        partner = T.cores[T.rank_of(home) ^ STEP[r]]
        data, lst = relays(home, partner, topo)
        rid, pid = topo.addr(partner, core) if core in data or core == lst else (0, 0)
        es = topo.engines(core, partner)
        if core in data:
            k = data.index(core)
            n_in = len(topo.engines(home, core)) // 2
            a, b = k * HALF, (k + 1) * HALF
            g.wait_ge(T.sem["rc%d" % r], n_in)
            g.remote_dma(T["aq%d" % r][:, a:b].bitcast(dt.uint8), T["aq%d" % r][:, a:b].bitcast(dt.uint8), T.sem["aq_%d" % r], T.sem.left, pid, rid, bits(es))
            g.wait_ge(T.sem["rs%d" % r], n_in)
            g.remote_dma(T["ap%d" % r][:, a:b], T["ap%d" % r][:, a:b], T.sem["aq_%d" % r], T.sem.left, pid, rid, bits(es))
            left += 2 * len(es)
        if core == lst:
            g.wait_ge(T.sem["rL%d" % r], len(topo.engines(home, core)))
            g.remote_dma(T["al%d" % r][:], T["al%d" % r][:], T.sem["aL_%d" % r], T.sem.left, pid, rid, bits(es))
            left += len(es)
    if left:
        g.wait_ge(T.sem.left, left)


def rank_program(g, core, T, topo):
    rank = T.rank_of(core)
    if rank is None:
        return relay_program(g, core, T, topo)
    A = AluOpType
    F = ActivationFunctionType
    queue = {"v": g.vector, "a": g.scalar, "t": g.tensor, "g": g, "s": g.sync}
    own = {"v": "sv", "a": "sa", "t": "st", "g": "sg"}
    known = {e: {} for e in queue}
    count, snap, wr, rd = {}, {}, {}, {}

    def need(e, deps):
        deps = [d for d in set(deps) if known[e].get(d[0], 0) < d[1]]
        deps.sort(key=lambda d: -sum(snap.get(d, {}).values()))
        for d in deps:
            if known[e].get(d[0], 0) >= d[1]:
                continue
            queue[e].wait_ge(T.sem[d[0]], d[1])
            for s, n in list(snap.get(d, {}).items()) + [d]:
                known[e][s] = max(known[e].get(s, 0), n)

    def before(e, reads, writes):
        deps = []
        for k in reads:
            deps += wr.get(k, [])
        for k in writes:
            deps += wr.get(k, []) + rd.get(k, [])
        need(e, deps)

    def after(reads, writes, d):
        for k in reads:
            rd[k] = [x for x in rd.get(k, []) if x[0] != d[0]] + [d]
        for k in writes:
            wr[k] = [d]
            rd[k] = []

    def op(e, reads, writes, call):
        before(e, reads, writes)
        s = own[e]
        count[s] = count.get(s, 0) + 1
        call().then_inc(T.sem[s], 1)
        d = (s, count[s])
        snap[d] = dict(known[e])
        snap[d][s] = count[s]
        after(reads, writes, d)

    def dma(e, sem, total, reads, writes, out, in_):
        before(e, reads, writes)
        queue[e].dma_start(out, in_).then_inc(T.sem[sem], 16)
        count[sem] = 16 * total
        d = (sem, 16 * total)
        m = snap.setdefault(d, {})
        for s, n in known[e].items():
            m[s] = max(m.get(s, 0), n)
        for k in reads:
            rd[k] = [x for x in rd.get(k, []) if x != d] + [d]
        for k in writes:
            wr[k] = [x for x in wr.get(k, []) if x == d] or [d]
            rd[k] = []

    def ts(reads, writes, out, in0, s1, op0, s2=None, op1=None):
        if op1 is None:
            op("v", reads, writes, lambda: g.vector.tensor_scalar(out, in0, s1, None, op0))
        else:
            op("v", reads, writes, lambda: g.vector.tensor_scalar(out, in0, s1, s2, op0, op1))

    def tt(reads, writes, out, in0, in1, o):
        op("v", reads, writes, lambda: g.vector.tensor_tensor(out, in0, in1, o))

    def cp(reads, writes, out, in_):
        op("v", reads, writes, lambda: g.vector.tensor_copy(out, in_))

    def act(reads, writes, out, in_, f=F.Copy, **kw):
        op("a", reads, writes, lambda: g.scalar.activation(out, in_, f, **kw))

    def mm(reads, bank, lhs, lhsp, rhs, rhsp):
        op("t", reads, ["ps%d" % bank], lambda: g.tensor.matmul_mx(T["ps%d" % bank][:, 0:C], lhs, lhsp, rhs, rhsp, True, True))

    def quant(reads, writes, q, p, t):
        op("v", reads, writes, lambda: g.vector.quantize_mx(q, p, t))

    def fill(key, ap, c):
        op("v", [], [key], lambda: g.vector.memset(ap, c))

    dma("s", "lp", 1, [], ["pI"], T.pI[:], T.pg[:])
    dma("a", "lk", 1, [], ["kI"], T.kI[:], T.kg[:])
    dma("s", "lx", 1, [], ["xt"], T.xt[:], T.x[:])
    dma("a", "lu", 1, [], ["ut"], T.ut[:], T.u[:])
    dma("a", "lm", 1, [], ["mI"], T.mI[:], T.mg[:])
    dma("s", "lw", 1, [], ["wq"], T.wq[:].bitcast(dt.uint8), T.wc[:])
    dma("s", "lws", 1, [], ["wp"], T.wp[:], T.ws[:])
    dma("a", "lv", 1, [], ["vt"], T.vt[:], T.v[:])

    op("g", [], ["pid0"], lambda: g.iota(T.pid[:, 0:1], [[0, 1]], 0, 1))
    op("g", [], ["ior"], lambda: g.iota(T.ior[:], [[1, C]], -144, 0, allow_small_or_imprecise_dtypes=True))
    op("g", [], ["ulf"], lambda: g.iota(T.ulf[:, 0:16], [[64, 2], [32, 4], [0, 2]], -96, 0, allow_small_or_imprecise_dtypes=True))
    op("g", [], ["ulf2"], lambda: g.iota(T.ulf[:, 16:24], [[16, 8]], 0, 0, allow_small_or_imprecise_dtypes=True))
    fill("ones", T.ones[:], 1.0)
    op("g", ["ones"], ["e0"], lambda: g.affine_select(T.e0[:], T.ones[:], [[1, 516]], A.is_equal, 0.0, -3, -4))
    S, I = T.cst, T.pid
    cc = lambda j: S[:, j:j + 1]

    def plain(key, out, n, c):
        act(["ones"], [key], out, T.ones[:, 0:n], scale=c)

    fill("ke", T.ke[:], 0.0)
    fill("ko", T.ko[:], 0.0)
    plain("pr0", T.pr0[:, 0:2 * C:2], C, 0.0)
    for i in (1, 2, 3, 0):
        plain("tr%da" % i, T["tr%d" % i][:, 16:32], 16, 0.0)
        plain("tr%db" % i, T["tr%d" % i][:, 352:368], 16, 0.0)
    ts(["pid0"], ["pid1"], I[:, 1:2], I[:, 0:1], 3, A.bitwise_and)
    ts(["pid0"], ["pid2"], I[:, 2:3], I[:, 0:1], 2, A.logical_shift_right, 3, A.bitwise_and)
    ts(["pid0"], ["pid3"], I[:, 3:4], I[:, 0:1], 4, A.logical_shift_right, 1, A.bitwise_and)
    ts(["pid0"], ["pid4"], I[:, 4:5], I[:, 0:1], 5, A.logical_shift_right)
    ts(["pid3"], ["c3"], cc(3), I[:, 3:4], 0.0, A.is_equal)
    cp(["pid3"], ["c4"], cc(4), I[:, 3:4])
    ts(["ior"], ["idr"], T.idr[:], T.ior[:], 0.25, A.mult)
    cp(["pid1"], ["c0"], cc(0), I[:, 1:2])
    ts(["pid2"], ["c1"], cc(1), I[:, 2:3], 2.0, A.is_equal)
    ts(["c0", "c1"], ["c7"], cc(7), cc(0), 16.0, A.mult, cc(1), A.add)
    ts(["ulf", "c7"], ["ull"], T.ull[:, 0:16], T.ulf[:, 0:16], cc(7), A.add, 0.0, A.max)
    cp(["ulf2"], ["ull2"], T.ull[:, 16:24], T.ulf[:, 16:24])

    cp(["kI"], ["kf"], T.kf[:], T.kI[:])
    cp(["pI"], ["pls"], T.pls[:], T.pI[:])
    ts(["pI"], ["tl1"], T.tl1[:, 0:18], T.pI[:], 2.0, A.mult, 1.0, A.add)
    cp(["idr", "pls", "pr0"], ["pr0"], T.pr0[:, 1:2 * C:2], T.idr[:].indirect(T.pls[:]))
    for h in range(2):
        for y in range(2):
            c0 = 10 * (1 - h) + y
            n = len(range(c0, 18 if h == 0 else 10, 2))
            m0 = 2 * h + y
            act(["kf", "c3", "ke"], ["ke%d" % m0], T.ke[:, m0:m0 + 4 * n - 3:4], T.kf[:, c0:c0 + 2 * n - 1:2], scale=cc(3))
    act(["kf", "c4", "ko"], ["ko1"], T.ko[:, 1:20:2], T.kf[:, 0:10], scale=cc(4))
    act(["kf", "c4", "ko"], ["ko0"], T.ko[:, 0:15:2], T.kf[:, 10:18], scale=cc(4))
    tt(["ke0", "ke1", "ke2", "ke3", "ko0", "ko1"], ["ke"], T.ke[:], T.ke[:], T.ko[:], A.add)
    ts(["ke"], ["k20"], T.k20[:], T.ke[:], 2.0, A.mult, 1.0, A.add)
    cp(["ke"], ["k20p"], T.k20p[:], T.ke[:])
    cp(["pr0", "tl1"], ["pr1"], T.pr1[:, 0:C], T.pr0[:].indirect(T.tl1[:, 0:18]))
    act(["pr0", "k20"], ["tr1"], T.tr1[:, 32:352], T.pr0[:].indirect(T.k20[:]))
    act(["pr1", "k20p"], ["tr2"], T.tr2[:, 32:352], T.pr1[:, 0:C].indirect(T.k20p[:]))
    act(["idr", "k20p"], ["tr0"], T.tr0[:, 32:352], T.idr[:].indirect(T.k20p[:]))
    plain("tab", T.tab[:], 8 * BLK, 0.0)
    act(["c3", "ones"], ["m42"], T.m42[:, 0:42:2], T.ones[:, 0:21], scale=cc(3))
    act(["c4", "ones"], ["m42b"], T.m42[:, 1:42:2], T.ones[:, 0:21], scale=cc(4))
    act(["pr0"], ["pd1"], T.pd[:, 1:2 * C:2], T.pr0[:, 1:2 * C:2])
    plain("cg0", T.cg[:, 0:BLK:4], ENT, 0.0)
    plain("cg1", T.cg[:, 1:BLK:4], ENT, 1.0)
    plain("cg2", T.cg[:, 2:BLK:4], ENT, -1.0)
    plain("cg3", T.cg[:, 3:BLK:4], ENT, 1.0)
    plain("c14", cc(14), 1, -1e-29)
    plain("tb6", T.tb6[:], 48, 0.0)
    plain("tb7", T.tb7[:], 48, 0.0)
    for i in range(2):
        plain("gg%da" % i, T["gg%d" % i][:, 16:32], 16, 0.0)
        plain("gg%db" % i, T["gg%d" % i][:, 192:208], 16, 0.0)
    plain("ne0", T.ne2[:, 0:2 * C:2], C, 0.0)

    def turn(n):
        k, t = "tr%d" % n, "tt%d" % n
        op("v", [k], [t + "a"], lambda: g.vector.transpose(T[t][:, 0:320], T[k][:, 32:352]))
        op("v", [k, k + "a", k + "b"], [t + "b"], lambda: g.vector.transpose(T[t][:, 320:672], T[k][:, 16:368]))

    def ent(n):
        return T["tt%d" % n][:, 0:672:16]

    def aslist(n, name):
        t = "tt%d" % n
        tt([t + "a", t + "b", "m42", "m42b"], ["xm"], T.xm[:], ent(n), T.m42[:], A.mult)
        tt(["xm"], ["lf"], T.lf[:], T.xm[:, 0:20], T.xm[:, 21:41], A.add)
        ts(["lf"], [name], T[name][:], T.lf[:], 8.0, A.mult, 2 * BIAS + 1, A.add)

    def rows(n, key, lst, e="v"):
        (cp if e == "v" else act)([key, lst], ["tr%d" % n], T["tr%d" % n][:, 32:352], T[key][:].indirect(T[lst][:]))

    COMB = [("cR", "cU", A.subtract), ("cP", "cQ", A.subtract), ("cR", "cU", A.add), ("cP", "cQ", A.add)]

    def powers(r):
        p = "pr%d" % r
        rows(1, p, "k20")
        turn(1)
        aslist(1, "tl1")
        rows(2, p, "tl1")
        turn(2)
        aslist(2, "tl2")
        middle()

    def middle():
        ks = ["tt1a", "tt1b", "tt2a", "tt2b"]
        tt(ks, ["cQ"], T.cQ[:], ent(1), ent(2), A.add)
        tt(ks, ["cU"], T.cU[:], ent(1), ent(2), A.subtract)

    def tables(r):
        turn(3)
        ks = ["tt0a", "tt0b", "tt3a", "tt3b"]
        tt(ks, ["cP"], T.cP[:], ent(0), ent(3), A.add)
        tt(ks, ["cR"], T.cR[:], ent(3), ent(0), A.subtract)
        for h in range(2):
            for k in range(4):
                x, y, o = COMB[k]
                c0 = 6 * BLK + BLK * h + k
                tt([x, y], ["tab"] if h == k == 0 else ["tab%d" % (4 * h + k)], T.tab[:, c0:c0 + BLK - 3:4], T[x][:, h:20:2], T[y][:, h:20:2], o)
        ks = ["tab"] + ["tab%d" % i for i in range(1, 8)]
        for b in range(4):
            for a in range(b):
                c0 = 6 * BLK - 2 * BLK * (b - a)
                dma("s", "dt%d" % r, 6, ks, ["far%d%d" % (a, b)], T.tab[32 * b:32 * b + 32, c0:c0 + 2 * BLK], T.tab[32 * a:32 * a + 32, 6 * BLK:8 * BLK])

    def tail(i):
        k = i % 4
        x, y, o = COMB[k]
        if i < 4:
            tt([x, y, "tb6"], ["tb6_%d" % k], T.tb6[:, 4 + k:4 + k + 41:4], T[x][:, 20:42:2], T[y][:, 20:42:2], o)
        else:
            tt([x, y, "tb7"], ["tb7_%d" % k], T.tb7[:, k:k + 41:4], T[x][:, 21:42:2], T[y][:, 21:42:2], o)

    def ends():
        act(["c4"] + ["tab%d" % i for i in range(4, 8)], ["tfa"], T.tf[:, 0:40], T.tab[:, 7 * BLK:8 * BLK], scale=cc(4))
        act(["c4", "tb7"] + ["tb7_%d" % k for k in range(4)], ["tfb"], T.tf[:, 40:88], T.tb7[:], scale=cc(4))

    cp(["pr1", "pls"], ["pr2"], T.pr2[:, 0:C], T.pr1[:, 0:C].indirect(T.pls[:]))
    cp(["pr2", "k20p"], ["tr3"], T.tr3[:, 32:352], T.pr2[:, 0:C].indirect(T.k20p[:]))
    turn(1)
    turn(2)
    middle()
    turn(0)
    tables(0)

    quant(["xt"], ["q0", "qp0"], T.q0[:], T.qp0[:], T.xt[:])
    quant(["ut"], ["uq", "up"], T.uq[:], T.up[:], T.ut[:])
    cp(["uq", "ull", "ull2"], ["u3q"], T.u3q[:].bitcast(dt.uint32), T.uq[:].bitcast(dt.uint32).indirect(T.ull[:]))
    act(["up", "ull", "ull2"], ["u3p"], T.u3p[:], T.up[:].indirect(T.ull[:]))
    ts(["pid2"], ["c2"], cc(2), I[:, 2:3], 0.0, A.not_equal)
    ts(["pid4", "c0"], ["c5"], cc(5), I[:, 4:5], 2.0, A.mult, cc(0), A.add)
    ts(["c1"], ["c6"], cc(6), cc(1), -2.0, A.mult, 1.0, A.add)
    for w in range(2):
        ts(["c5", "c2"], ["c%d" % (8 + w)], cc(8 + w), cc(5), 5.0 - 4 * w, A.not_equal, cc(2), A.mult)
        ts(["c5", "c6"], ["c%d" % (10 + w)], cc(10 + w), cc(5), 5.0 - 4 * w, A.is_equal, cc(6), A.mult)
        ts(["c2", "c%d" % (10 + w)], ["c%d" % (12 + w)], cc(12 + w), cc(10 + w), -1e-29, A.add, cc(2), A.mult)
    cp(["mI"], ["mls"], T.mls[:], T.mI[:])
    ts(["mI"], ["m2"], T.m2[:], T.mI[:], 2.0, A.mult, 1.0, A.add)

    def unit(b):
        quant(["e0"], ["eq%d" % b], T.eq[:, 128 * b:128 * b + 128], T.ep[:, 128 * b:128 * b + 128], T.e0[:, 3 - b:515 - b])

    unit(0)
    unit(1)

    left = [0]
    for r in range(3):
        partner = T.cores[rank ^ STEP[r]]
        data, lst = relays(core, partner, topo)
        q, qp, p = "q%d" % r, "qp%d" % r, "pr%d" % r
        need("g", wr[q])
        fc, fs = [], []
        for k, c in enumerate(data):
            es = topo.engines(core, c)
            es = es[k * len(es) // 2:(k + 1) * len(es) // 2]
            rid, pid = topo.addr(c, core)
            a, b = k * HALF, (k + 1) * HALF
            fc.append(RemoteDMATransfer(dst_ids=[DstId(rid=rid, pnc=pid)], dma_engine_mask=bits(es), remote_sem=T.sem["rc%d" % r],
                                        src=T[q][:, a:b].bitcast(dt.uint8), dst=T["aq%d" % r][:, a:b].bitcast(dt.uint8)))
            fs.append(RemoteDMATransfer(dst_ids=[DstId(rid=rid, pnc=pid)], dma_engine_mask=bits(es), remote_sem=T.sem["rs%d" % r],
                                        src=T[qp][:, a:b], dst=T["ap%d" % r][:, a:b]))
            left[0] += 2 * len(es)
        g.remote_dma_fused(fc, local_sem=T.sem.left)
        g.remote_dma_fused(fs, local_sem=T.sem.left)
        for w in range(3):
            mm([q, qp, "u3q", "u3p"], w, T.u3q[:, 128 * w:128 * w + 128], T.u3p[:, 128 * w:128 * w + 128], T[q][:], T[qp][:])

        def own_f(b):
            mm([q, qp, "eq%d" % b], 3 + b, T.eq[:, 128 * b:128 * b + 128], T.ep[:, 128 * b:128 * b + 128], T[q][:], T[qp][:])

        for b in range(4 if r else 2):
            own_f(b)

        def signs(w):
            act(["ps%d" % w, "c%d" % (8 + w), "c%d" % (12 + w)], ["w%d" % (w + 1)], T["w%d" % (w + 1)][:], T["ps%d" % w][:, 0:C], F.Sign, scale=cc(8 + w), bias=cc(12 + w))

        def meanwhile(t):
            if t == 0:
                signs(1)
            elif t == 1:
                act(["ps2", "c14"], ["wg"], T.wg[:], T.ps2[:, 0:C], F.Sign, bias=cc(14))
            elif t in (2, 3, 7, 8):
                b = (2, 3, 7, 8).index(t)
                act(["ps%d" % (3 + b)], ["fo%d" % b], T["fo%d" % b][:], T["ps%d" % (3 + b)][:, 0:C])
            elif t == 4:
                ends()

        signs(0)
        def differ():
            tt([p, "pd1", "m2"], ["pd0"], T.pd[:, 0:2 * C:2], T[p][:].indirect(T.m2[:]), T.pd[:, 1:2 * C:2], A.subtract)

        if r:
            differ()
        far = ["far%d%d" % (a, b) for b in range(4) for a in range(b)]
        scan = lambda out, d0, d1: (lambda: g.vector.tensor_tensor_scan(out, d0, d1, 0.0, A.mult, A.add))
        op("v", ["cg0", "cg1", "cg2", "cg3", "tab"] + far, ["sc0"], scan(T.sc0[:], T.cg[:], T.tab[:, 0:BLK]))
        ts(["sc0"], ["of0"], T.of0[:], T.sc0[:, 3:BLK:4], BIAS, A.add)
        for t in range(7):
            i, j = t % 2, (t + 1) % 2
            w, lane = "w%d" % (1 + t // 4), t % 4
            gg, gt = "gg%d" % i, "gt%d" % i
            cp([w, "of%d" % i], [gg], T[gg][:, 32:128], T[w][:].indirect(T["of%d" % i][:, 0:6]))
            act([w, "of%d" % i], [gg + "s"], T[gg][:, 128:192], T[w][:].indirect(T["of%d" % i][:, 6:10]))
            if t < 4:
                tail(2 * t)
            op("v", [gg, gg + "s"], [gt], lambda: g.vector.transpose(T[gt][:, 0:160], T[gg][:, 32:192]))
            if t < 4:
                tail(2 * t + 1)
            elif r == 0 and t < 6:
                unit(t - 2)
                own_f(t - 2)
            meanwhile(t)
            d1 = ["tab%d" % k for k in range(8)] + ["tab"] + far
            if t < 5:
                op("v", [gt] + d1, ["sc%d" % j], scan(T["sc%d" % j][:], T[gt][:, lane:160:4], T.tab[:, BLK * (t + 1):BLK * (t + 2)]))
                ts(["sc%d" % j], ["of%d" % j], T["of%d" % j][:], T["sc%d" % j][:, 3:BLK:4], BIAS, A.add)
            elif t == 5:
                op("v", [gt] + d1, ["s5"], scan(T.s5[:], T[gt][:, lane:160:4], T.tab[:, 6 * BLK:7 * BLK]))
                op("v", [gg, gg + "s", gg + "a", gg + "b"], [gt + "b"], lambda: g.vector.transpose(T[gt][:, 160:352], T[gg][:, 16:208]))
                ts(["s5"], ["of0"], T.of0[:], T.s5[:, 3:BLK:4], BIAS, A.add)
                op("v", [gt + "b", "tb6"] + ["tb6_%d" % k for k in range(4)], ["s5b"], scan(T.s5b[:], T[gt][:, 160 + lane:352:4], T.tb6[:]))
            else:
                act(["s5", "c3"], ["pm0"], T.pm[:, 0:10:2], T.s5[:, 7:40:8], scale=cc(3))
                act(["s5", "c3"], ["pm1"], T.pm[:, 10:18:2], T.s5[:, 3:32:8], scale=cc(3))
                act(["s5b", "c3"], ["pm2"], T.pm[:, 1:10:2], T.s5b[:, 15:48:8], scale=cc(3))
                act(["s5b", "c3"], ["pm3"], T.pm[:, 11:18:2], T.s5b[:, 11:36:8], scale=cc(3))
                op("v", [gg, gg + "s", gg + "a", gg + "b"], [gt + "b"], lambda: g.vector.transpose(T[gt][:, 160:352], T[gg][:, 16:208]))
                op("v", [gt, gt + "b", "tfa", "tfb"], ["s6"], scan(T.s6[:], T[gt][:, lane:352:4], T.tf[:]))
        ll = "ll%d" % r
        tt(["s6", "pm0", "pm1", "pm2", "pm3"], ["l32"], T.l32[:], T.s6[:, 3:72:4], T.pm[:], A.add)
        ts(["l32"], [ll], T[ll][:], T.l32[:], BIAS, A.add)
        need("g", wr[ll])
        rid, pid = topo.addr(lst, core)
        es = topo.engines(core, lst)
        g.remote_dma(T["al%d" % r][:], T[ll][:], T.sem["rL%d" % r], T.sem.left, pid, rid, bits(es))
        left[0] += len(es)
        np_ = "pr%d" % (r + 1)
        act(["wg", ll], ["be2"], T.be2[:], T.wg[:].indirect(T[ll][:]))
        meanwhile(7)
        meanwhile(8)
        cp(["wg", ll], ["be"], T.be[:], T.wg[:].indirect(T[ll][:]))
        if r == 0:
            differ()
        tt(["be", "be2", "mls"], ["ne1"], T.ne2[:, 1:2 * C:2], T.be[:].indirect(T.mls[:]), T.be2[:], A.not_equal)
        op("v", ["ne0", "ne1", "pd0", "pd1"], [np_], scan(T[np_][:], T.ne2[:], T.pd[:]))
        if r < 2:
            powers(r + 1)
        else:
            cp(["idr", ll], ["lo"], T.lo[:], T.idr[:].indirect(T[ll][:]))
            quant(["vt"], ["vq"], T.vq[:], T.vp[:], T.vt[:])
            ts(["lo"], ["lo"], T.lo[:], T.lo[:], 4.0, A.mult, BIAS, A.add)
            ts([np_], ["po"], T.po[:], T[np_][:, 1:2 * C:2], 4.0, A.mult, BIAS, A.add)
            dma("s", "out", 8, ["lo"], ["pl0"], T.pl[:, 0:C], T.lo[0:128:16, :])
            dma("s", "out", 8, ["po"], ["pl1"], T.pl[:, C:2 * C], T.po[0:128:16, :])
        wr["aq"] = [("aq_%d" % r, sum(2 * len(topo.engines(c, core)) for c in relays(partner, core, topo)[0]))]
        wr["al"] = [("aL_%d" % r, len(topo.engines(relays(partner, core, topo)[1], core)))]
        count["aq_%d" % r], count["aL_%d" % r] = wr["aq"][0][1], wr["al"][0][1]
        for b in range(4):
            mm(["aq", "eq%d" % b], (7 + b) % 8, T.eq[:, 128 * b:128 * b + 128], T.ep[:, 128 * b:128 * b + 128], T["aq%d" % r][:], T["ap%d" % r][:])
        for b in range(4):
            act(["ps%d" % ((7 + b) % 8)], ["fp%d" % b], T["fp%d" % b][:], T["ps%d" % ((7 + b) % 8)][:, 0:C])
        al, zt = T["al%d" % r], T.zt
        for b in (0, 2, 1, 3):
            if b < 2:
                cp(["fp%d" % b, "al"], ["zt%d" % b], zt[:, b:4 * C:4], T["fp%d" % b][:].indirect(al[:]))
            else:
                act(["fp%d" % b, "al"], ["zt%d" % b], zt[:, b:4 * C:4], T["fp%d" % b][:].indirect(al[:]))
        quant(["zt%d" % b for b in range(4)], ["zq"], T.zq[:], T.zp[:], zt[:])
        if r < 2:
            rows(3, np_, "tl2", "a")
            tables(r + 1)
        for b in range(4):
            mm(["zq", "wq", "wp"], 3 + b, T.wq[:, 128 * b:128 * b + 128], T.wp[:, 128 * b:128 * b + 128], T.zq[:], T.zp[:])
        xn = T["xn%d" % r]
        for b in range(4):
            act(["ps%d" % (3 + b)], ["hb%d" % b], T["hb%d" % b][:], T["ps%d" % (3 + b)][:, 0:C], scale=0.03125)
            tt(["hb%d" % b, "fo%d" % b, ll], ["xn%d" % b], xn[:, b:4 * C:4], T["hb%d" % b][:].indirect(T[ll][:]), T["fo%d" % b][:], A.add)
        if r < 2:
            act([np_], ["pd1"], T.pd[:, 1:2 * C:2], T[np_][:, 1:2 * C:2])
        nq, nqp = "q%d" % (r + 1), "qp%d" % (r + 1)
        quant(["xn%d" % b for b in range(4)], [nq, nqp], T[nq][:], T[nqp][:], xn[:])
    mm(["q3", "qp3", "vq"], 7, T.vq[:], T.vp[:], T.q3[:], T.qp3[:])
    dma("s", "out", 8, ["q3"], ["oc"], T.oc[:], T.q3[:].bitcast(dt.uint8))
    for k in range(4):
        dma("s" if k % 2 else "a", "out", 8, ["qp3"], ["osc%d" % k], T.osc[4 * k:4 * k + 4, :], T.qp3[32 * k:32 * k + 4, :])
    act(["ps7"], ["yo"], T.yo[:], T.ps7[:, 0:C])
    dma("s", "out", 8, ["yo"], ["y"], T.y[:], T.yo[:])
    g.wait_ge(T.sem.left, left[0])
    for s in sorted(count):
        g.wait_ge(T.sem[s], count[s])
